import numpy as np
import ml_dtypes


def mxq(x, axis, fmt="e4m3"):
    dtype, down = {"e4m3": (ml_dtypes.float8_e4m3fn, 7), "e5m2": (ml_dtypes.float8_e5m2, 14)}[fmt]
    v = np.moveaxis(np.asarray(x, np.float32).astype(ml_dtypes.bfloat16).astype(np.float64), axis, -1)
    blocks = v.reshape(v.shape[:-1] + (-1, 32))
    amax = np.abs(blocks).max(-1, keepdims=True)
    byte = np.maximum(np.where(amax > 0, np.frexp(amax)[1] - 1 + 127, 0) - down, 1)
    scale = np.exp2(byte - 127.0)
    codes = (blocks / scale).astype(np.float32).astype(dtype).astype(np.float64)
    return np.moveaxis((codes * scale).reshape(v.shape), -1, axis)


WIDE = False


def mx_kscale(k):
    if not WIDE:
        return np.ones(k)
    levels = np.array([18, -18])
    if k % 512:
        return np.exp2(np.random.permutation(np.resize(levels, k // 32))).repeat(32)
    a = np.empty((k // 512, 16))
    for p in range(k // 512):
        a[p, :8] = np.random.permutation(np.resize(levels, 8))
        for g in range(8):
            far = levels[np.abs(levels - a[p, g]) >= 10]
            a[p, g + 8] = far[np.random.randint(len(far))]
    return np.exp2(a.ravel()).repeat(32)


def f64(x):
    return np.asarray(x).astype(np.float64)


def striped(idx):
    return np.tile(np.asarray(idx).reshape(-1, 16).T, (8, 1)).astype(np.uint16)


def unstriped(offs):
    return offs[:16].T.reshape(-1).astype(np.int64)


E2M1 = np.array([0.0, 0.5, 1.0, 1.5, 2.0, 3.0, 4.0, 6.0, -0.0, -0.5, -1.0, -1.5, -2.0, -3.0, -4.0, -6.0])


def pack_weight(w, fmt):
    k, n = w.shape
    w = f64(np.asarray(w, np.float32).astype(ml_dtypes.bfloat16)).reshape(k // 32, 32, n)
    amax = np.abs(w).max(1)
    if fmt == "e4m3":
        byte = np.frexp(amax)[1] - 1 + 127 - 7
    else:
        mant, ex = np.frexp(amax / 6.0)
        byte = np.where(mant > 0.5, ex, ex - 1) + 127
    byte = np.clip(np.where(amax > 0, byte, 1), 1, 254)
    scaled = (w * np.exp2(127.0 - byte)[:, None, :]).reshape(k, n).astype(np.float32)
    by_word = np.ascontiguousarray(scaled.reshape(k // 512, 128, 4, n).transpose(0, 1, 3, 2))
    if fmt == "e4m3":
        words = by_word.astype(ml_dtypes.float8_e4m3fn).view(np.uint8)
    else:
        c = by_word.astype(ml_dtypes.float4_e2m1fn).view(np.uint8) & 0xF
        words = (c[..., 0::2] | (c[..., 1::2] << 4)).reshape(k // 512, 128, 2 * n)
    return np.ascontiguousarray(words), np.ascontiguousarray(byte.astype(np.uint8).reshape(k // 512, 16, n))


def unpack_weight(words, scales, fmt):
    g, _, n = scales.shape
    words = np.ascontiguousarray(words).reshape(g, 128, n, -1)
    if fmt == "e4m3":
        vals = words.view(ml_dtypes.float8_e4m3fn).astype(np.float64)
    else:
        nib = np.empty((g, 128, n, 4), np.uint8)
        nib[..., 0::2] = words & 0xF
        nib[..., 1::2] = words >> 4
        vals = E2M1[nib]
    vals = vals * np.repeat(np.exp2(scales.astype(np.float64) - 127.0), 8, axis=1)[..., None]
    return vals.transpose(0, 1, 3, 2).reshape(g * 512, n)


def planes(y):
    n, m = y.shape
    v = y.astype(np.float32).astype(ml_dtypes.bfloat16).astype(np.float64).reshape(n // 32, 32, m)
    top = np.abs(v).max(1)
    byte = np.clip(np.where(top > 0, np.frexp(top)[1] - 1 + 127 - 7, 1), 1, 254)
    codes = (v * np.exp2(127.0 - byte)[:, None, :]).reshape(n, m).astype(np.float32).astype(ml_dtypes.float8_e4m3fn).view(np.uint8)
    words = codes.reshape(n // 512, 128, 4, m).transpose(0, 1, 3, 2)
    return np.ascontiguousarray(words), np.ascontiguousarray(byte.astype(np.uint8).reshape(n // 512, 16, m))


def setup_inputs():
    n = np.random.standard_normal
    uni = np.random.uniform
    f0 = np.random.permutation(1024)[:512]
    f1 = np.random.permutation(1024)[:512]
    f2 = np.random.permutation(1024)[:512]
    f3 = np.random.permutation(1024)[:512]
    f_m = mx_kscale(512)
    W_ = pack_weight(n((512, 512)) / np.sqrt(512) * f_m[:, None], "e2m1")
    return {
        "W_words": W_[0],
        "W_scales": W_[1],
        "dyT": (n((512, 1024)) / f_m[:, None]).astype(np.float32),
        "w0": np.tile(uni(0.1, 0.5, 512), (128, 1)).astype(np.float32),
        "w1": np.tile(uni(0.1, 0.5, 512), (128, 1)).astype(np.float32),
        "w2": np.tile(uni(0.1, 0.5, 512), (128, 1)).astype(np.float32),
        "w3": np.tile(uni(0.1, 0.5, 512), (128, 1)).astype(np.float32),
        "f0offs": striped(f0),
        "f1offs": striped(f1),
        "f2offs": striped(f2),
        "f3offs": striped(f3),
    }


def reference(W_words, W_scales, dyT, w0, w1, w2, w3, f0offs, f1offs, f2offs, f3offs):
    f0 = unstriped(f0offs)
    f1 = unstriped(f1offs)
    f2 = unstriped(f2offs)
    f3 = unstriped(f3offs)
    W = unpack_weight(W_words, W_scales, "e2m1")
    u = W.T @ mxq(f64(dyT), 0, "e5m2")
    u0 = u[:, f0]
    u1 = u[:, f1]
    u2 = u[:, f2]
    u3 = u[:, f3]
    out_0 = f64(w0)[:1] * u0 + f64(w1)[:1] * u1 + f64(w2)[:1] * u2 + f64(w3)[:1] * u3
    return (out_0,) + planes(out_0)

@@ -1,0 +1,180 @@
+from contextlib import ExitStack
+
+import concourse.mybir as mybir
+from concourse.masks import make_identity
+
+M, D, X, S = 512, 512, 512, 1024
+FLOPS = 2 * M * D * S
+
+F32 = mybir.dt.float32
+BF16 = mybir.dt.bfloat16
+I32 = mybir.dt.int32
+U32 = mybir.dt.uint32
+U16 = mybir.dt.uint16
+U8 = mybir.dt.uint8
+E5M2 = mybir.dt.float8_e5m2_x4
+E4M3 = mybir.dt.float8_e4m3fn_x4
+E2M1 = mybir.dt.float4_e2m1fn_x4
+MULT = mybir.AluOpType.mult
+ADD = mybir.AluOpType.add
+
+P = 128
+PACK = 4
+N = 512
+DY_CHUNKS = (256, 256, 256, 256)
+WIDE = 384
+LAST = X - WIDE
+
+
+def tile_attend_gupsamp_pl_kernel(
+    tc, W_words, W_scales, dyT, w0, w1, w2, w3, f0offs, f1offs, f2offs, f3offs, out_0, out_1, out_2
+):
+    nc = tc.nc
+    with ExitStack() as ctx:
+        keep = ctx.enter_context(tc.tile_pool(name="keep", bufs=1))
+        psum = ctx.enter_context(tc.psum_pool(name="psum", bufs=4))
+
+        offs = [keep.tile([P, X // 16], U16, name="offs%d" % j) for j in range(4)]
+        w_raw = keep.tile([P, 2 * D], U8, name="w_raw", align_bytes=64)
+        ws_raw = keep.tile([P, D], U8, name="ws_raw", align_bytes=64)
+        w_dealt = keep.tile([P, 2 * D], U8, name="w_dealt", align_bytes=64)
+        ws_dealt = keep.tile([P, D], U8, name="ws_dealt", align_bytes=64)
+        ident = keep.tile([P, P], F32, name="ident")
+
+        nc.gpsimd.memset(ws_raw[:].bitcast(I32), 0)
+        nc.scalar.dma_start(out=w_raw[:].bitcast(I32), in_=W_words[0].bitcast(I32))
+        raws = []
+        s0 = 0
+        for k, width in enumerate(DY_CHUNKS):
+            raw = keep.tile([P, PACK, width], F32, name="stage%d" % k)
+            nc.sync.dma_start(out=raw[:], in_=dyT[:, s0 : s0 + width].rearrange("(p j) w -> p j w", j=PACK))
+            raws.append((raw, s0, width))
+            s0 = s0 + width
+            if k == 0:
+                for q in range(4):
+                    nc.sync.dma_start(
+                        out=ws_raw[32 * q : 32 * q + 4, :].bitcast(I32),
+                        in_=W_scales[0, 4 * q : 4 * q + 4, :].bitcast(I32),
+                    )
+        for j, f in enumerate((f0offs, f1offs, f2offs, f3offs)):
+            nc.sync.dma_start(offs[j][:], f)
+        make_identity(nc, ident[:])
+
+        nc.vector.tensor_copy(
+            out=w_dealt[:].bitcast(U16).rearrange("p (t q) -> p t q", t=PACK),
+            in_=w_raw[:].bitcast(U16).rearrange("p (q t) -> p t q", t=PACK),
+        )
+        nc.vector.tensor_copy(
+            out=ws_dealt[:].rearrange("p (t q) -> p t q", t=PACK),
+            in_=ws_raw[:].rearrange("p (q t) -> p t q", t=PACK),
+        )
+
+        codes = [keep.tile([P, N], U32, name="dy_codes%d" % h, align_bytes=64) for h in range(2)]
+        scales = [keep.tile([P, N], U8, name="dy_scales%d" % h, align_bytes=64) for h in range(2)]
+        u = [keep.tile([P, S], F32, name="u%d" % t) for t in range(PACK)]
+        for k, (raw, s0, width) in enumerate(raws):
+            grouped = keep.tile([P, width, PACK], BF16, name="dy_bf%d" % k, align_bytes=64)
+            nc.vector.tensor_copy(out=grouped[:], in_=raw[:].rearrange("p j w -> p w j"))
+            h, c0 = divmod(s0, N)
+            nc.vector.quantize_mx(
+                out=codes[h][:, c0 : c0 + width].bitcast(E5M2),
+                scales=scales[h][:, c0 : c0 + width],
+                in_=grouped[:].rearrange("p w j -> p (w j)"),
+            )
+        for t in range(PACK):
+            for h in range(2):
+                bank = psum.tile([P, N], F32, name="work")
+                nc.tensor.matmul_mx(
+                    out=bank[:],
+                    lhsT=w_dealt[:, 2 * P * t : 2 * P * (t + 1)].bitcast(E2M1),
+                    lhsT_scale=ws_dealt[:, P * t : P * (t + 1)],
+                    rhs=codes[h][:].bitcast(E5M2),
+                    rhs_scale=scales[h][:],
+                    start=True,
+                    stop=True,
+                )
+                nc.scalar.copy(out=u[t][:, N * h : N * (h + 1)], in_=bank[:])
+
+        wts = []
+        for k, pair in enumerate(((w0, w1), (w2, w3))):
+            both = keep.tile([P, 2, X], F32, name="stage%d" % k)
+            for e, w in enumerate(pair):
+                nc.sync.dma_start(out=both[:, e, :], in_=w)
+                wts.append(both[:, e, :])
+
+        y_codes = keep.tile([P, X], U32, name="y_codes", align_bytes=64)
+        y_scales = keep.tile([P, X], U8, name="y_scales", align_bytes=64)
+        out_rows = out_0.rearrange("(p t) x -> p t x", t=PACK)
+        out_words = out_1[0].rearrange("p x t -> p (x t)").bitcast(I32)
+
+        def product(t, j, x0, width):
+            prod = keep.tile([P, width], F32, name="prod%d_%d_%d" % (x0, t, j))
+            nc.vector.tensor_tensor(
+                prod[:],
+                u[t][:].indirect(offs[j][:, x0 // 16 : (x0 + width) // 16]),
+                wts[j][:, x0 : x0 + width],
+                MULT,
+            )
+            return prod
+
+        def add_turned(slot, prod_cols, j):
+            nc.tensor.matmul(slot, prod_cols, ident[:], start=(j == 0), stop=(j == 3), is_transpose=True)
+
+        def quantise(y_bf, x0):
+            nc.vector.quantize_mx(
+                out=y_codes[:, x0 : x0 + P].bitcast(E4M3),
+                scales=y_scales[:, x0 : x0 + P],
+                in_=y_bf[:].rearrange("p x t -> p (x t)"),
+            )
+
+        chunks = WIDE // P
+        turned = [psum.tile([P, PACK, P], F32, name="work") for c in range(chunks)]
+        for t in range(PACK):
+            for j in range(4):
+                prod = product(t, j, 0, WIDE)
+                for c in range(chunks):
+                    add_turned(turned[c][:, t, :], prod[:, P * c : P * (c + 1)], j)
+        y = keep.tile([P, PACK, WIDE], F32, name="y_wide")
+        for c in range(chunks):
+            y_turned = keep.tile([P, PACK, P], F32, name="y_turned%d" % c)
+            nc.scalar.copy(out=y_turned[:], in_=turned[c][:])
+            back = psum.tile([P, PACK, P], F32, name="back")
+            for t in range(PACK):
+                nc.tensor.transpose(back[:, t, :], y_turned[:, t, :], ident[:])
+            y_bf = keep.tile([P, P, PACK], BF16, name="y_bf%d" % c, align_bytes=64)
+            nc.scalar.copy(out=y_bf[:], in_=back[:].rearrange("p t x -> p x t"))
+            nc.scalar.copy(out=y[:, :, P * c : P * (c + 1)], in_=back[:])
+            quantise(y_bf, P * c)
+        nc.sync.dma_start(out=out_rows[:, :, 0:WIDE], in_=y[:])
+        nc.sync.dma_start(out=out_words[:, 0:WIDE], in_=y_codes[:, 0:WIDE].bitcast(I32))
+
+        y = keep.tile([P, PACK, LAST], F32, name="y_last")
+        for t in range(PACK - 1):
+            turned_t = psum.tile([P, P], F32, name="work")
+            for j in range(4):
+                add_turned(turned_t[:], product(t, j, WIDE, LAST)[:], j)
+            y_turned = keep.tile([P, P], F32, name="y_turned_last%d" % t)
+            nc.scalar.copy(out=y_turned[:], in_=turned_t[:])
+            back = psum.tile([P, P], F32, name="back")
+            nc.tensor.transpose(back[:], y_turned[:], ident[:])
+            nc.scalar.copy(out=y[:, t, :], in_=back[:])
+        nc.scalar.dma_start(out=out_rows[:, 0 : PACK - 1, WIDE:X], in_=y[:, 0 : PACK - 1, :])
+        t = PACK - 1
+        p0 = product(t, 0, WIDE, LAST)
+        p1 = product(t, 1, WIDE, LAST)
+        p2 = product(t, 2, WIDE, LAST)
+        nc.vector.tensor_tensor(p0[:], p0[:], p1[:], ADD)
+        p3 = product(t, 3, WIDE, LAST)
+        nc.vector.tensor_tensor(p0[:], p0[:], p2[:], ADD)
+        nc.vector.tensor_tensor(y[:, t, :], p0[:], p3[:], ADD)
+        nc.sync.dma_start(out=out_rows[:, t, WIDE:X], in_=y[:, t, :])
+        y_bf = keep.tile([P, P, PACK], BF16, name="y_bf_last", align_bytes=64)
+        nc.vector.tensor_copy(out=y_bf[:], in_=y[:].rearrange("p t x -> p x t"))
+        quantise(y_bf, WIDE)
+        nc.sync.dma_start(out=out_words[:, WIDE:X], in_=y_codes[:, WIDE:X].bitcast(I32))
+        for q in range(4):
+            queue = nc.sync if q % 2 == 0 else nc.scalar
+            queue.dma_start(
+                out=out_2[0, 4 * q : 4 * q + 4, :].bitcast(I32),
+                in_=y_scales[32 * q : 32 * q + 4, :].bitcast(I32),
+            )

@@ -17,13 +17,18 @@ E4M3 = mybir.dt.float8_e4m3fn_x4
 E2M1 = mybir.dt.float4_e2m1fn_x4
 MULT = mybir.AluOpType.mult
 ADD = mybir.AluOpType.add
+COPY = mybir.ActivationFunctionType.Copy
 
 P = 128
 PACK = 4
 N = 512
 DY_CHUNKS = (256, 256, 256, 256)
-WIDE = 384
-LAST = X - WIDE
+GROUPS = (256, 128, 128)
+LAST = GROUPS[-1]
+RING = 6
+TURN_BANKS = 3
+BACK_BANKS = 4
+LAG = 0
 
 
 def tile_attend_gupsamp_pl_kernel(
@@ -32,7 +37,7 @@ def tile_attend_gupsamp_pl_kernel(
     nc = tc.nc
     with ExitStack() as ctx:
         keep = ctx.enter_context(tc.tile_pool(name="keep", bufs=1))
-        psum = ctx.enter_context(tc.psum_pool(name="psum", bufs=4))
+        psum = ctx.enter_context(tc.psum_pool(name="psum", bufs=1))
 
         offs = [keep.tile([P, X // 16], U16, name="offs%d" % j) for j in range(4)]
         w_raw = keep.tile([P, 2 * D], U8, name="w_raw", align_bytes=64)
@@ -58,7 +63,11 @@ def tile_attend_gupsamp_pl_kernel(
                     )
         for j, f in enumerate((f0offs, f1offs, f2offs, f3offs)):
             nc.sync.dma_start(offs[j][:], f)
+        w_rows = keep.tile([P, P], F32, name="w_rows")
         make_identity(nc, ident[:])
+        nc.scalar.activation(w_rows[:], ident[:], COPY, scale=0.0)
+        for j, w in enumerate((w0, w1, w2, w3)):
+            nc.sync.dma_start(out=w_rows[4 * j : 4 * j + 4, :], in_=w[0].rearrange("(c x) -> c x", x=P))
 
         nc.vector.tensor_copy(
             out=w_dealt[:].bitcast(U16).rearrange("p (t q) -> p t q", t=PACK),
@@ -83,7 +92,7 @@ def tile_attend_gupsamp_pl_kernel(
             )
         for t in range(PACK):
             for h in range(2):
-                bank = psum.tile([P, N], F32, name="work")
+                bank = psum.tile([P, N], F32, name=("work%d" % (t % TURN_BANKS) if h else "back%d" % (t % BACK_BANKS)))
                 nc.tensor.matmul_mx(
                     out=bank[:],
                     lhsT=w_dealt[:, 2 * P * t : 2 * P * (t + 1)].bitcast(E2M1),
@@ -95,83 +104,103 @@ def tile_attend_gupsamp_pl_kernel(
                 )
                 nc.scalar.copy(out=u[t][:, N * h : N * (h + 1)], in_=bank[:])
 
-        wts = []
-        for k, pair in enumerate(((w0, w1), (w2, w3))):
-            both = keep.tile([P, 2, X], F32, name="stage%d" % k)
-            for e, w in enumerate(pair):
-                nc.sync.dma_start(out=both[:, e, :], in_=w)
-                wts.append(both[:, e, :])
+        w3_last = keep.tile([P, LAST], F32, name="stage0")
+        nc.sync.dma_start(out=w3_last[:], in_=w3[:, X - LAST : X])
+        w_bank = psum.tile([P, P], F32, name="back%d" % (BACK_BANKS - 1))
+        nc.tensor.transpose(w_bank[:], w_rows[:], ident[:])
+        w_cols = keep.tile([P, 16], F32, name="w_cols")
+        nc.scalar.activation(w_cols[:], w_bank[:, 0:16], COPY)
 
         y_codes = keep.tile([P, X], U32, name="y_codes", align_bytes=64)
         y_scales = keep.tile([P, X], U8, name="y_scales", align_bytes=64)
         out_rows = out_0.rearrange("(p t) x -> p t x", t=PACK)
         out_words = out_1[0].rearrange("p x t -> p (x t)").bitcast(I32)
 
-        def product(t, j, x0, width):
-            prod = keep.tile([P, width], F32, name="prod%d_%d_%d" % (x0, t, j))
-            nc.vector.tensor_tensor(
-                prod[:],
-                u[t][:].indirect(offs[j][:, x0 // 16 : (x0 + width) // 16]),
-                wts[j][:, x0 : x0 + width],
-                MULT,
-            )
-            return prod
+        gathered = []
+        units = []
+        later = []
 
-        def add_turned(slot, prod_cols, j):
-            nc.tensor.matmul(slot, prod_cols, ident[:], start=(j == 0), stop=(j == 3), is_transpose=True)
+        def listed(t, j, x0, width):
+            return u[t][:].indirect(offs[j][:, x0 // 16 : (x0 + width) // 16])
 
-        def quantise(y_bf, x0):
+        def gather(t, j, x0, width):
+            got = keep.tile([P, width], F32, name="ring%d" % (len(gathered) % RING))
+            gathered.append(got)
+            nc.vector.tensor_copy(got[:], listed(t, j, x0, width))
+            return got
+
+        def turn_bank(planes):
+            bank = psum.tile([P, planes, P], F32, name="work%d" % (len(units) % TURN_BANKS))
+            units.append(bank)
+            return bank
+
+        def quantise(y_bf, xc):
             nc.vector.quantize_mx(
-                out=y_codes[:, x0 : x0 + P].bitcast(E4M3),
-                scales=y_scales[:, x0 : x0 + P],
+                out=y_codes[:, xc : xc + P].bitcast(E4M3),
+                scales=y_scales[:, xc : xc + P],
                 in_=y_bf[:].rearrange("p x t -> p (x t)"),
             )
+            nc.sync.dma_start(out=out_words[:, xc : xc + P], in_=y_codes[:, xc : xc + P].bitcast(I32))
 
-        chunks = WIDE // P
-        turned = [psum.tile([P, PACK, P], F32, name="work") for c in range(chunks)]
-        for t in range(PACK):
-            for j in range(4):
-                prod = product(t, j, 0, WIDE)
-                for c in range(chunks):
-                    add_turned(turned[c][:, t, :], prod[:, P * c : P * (c + 1)], j)
-        y = keep.tile([P, PACK, WIDE], F32, name="y_wide")
-        for c in range(chunks):
-            y_turned = keep.tile([P, PACK, P], F32, name="y_turned%d" % c)
-            nc.scalar.copy(out=y_turned[:], in_=turned[c][:])
-            back = psum.tile([P, PACK, P], F32, name="back")
-            for t in range(PACK):
-                nc.tensor.transpose(back[:, t, :], y_turned[:, t, :], ident[:])
-            y_bf = keep.tile([P, P, PACK], BF16, name="y_bf%d" % c, align_bytes=64)
+        def turn_back(back, src, planes, first, last):
+            for i, t in enumerate(planes):
+                nc.tensor.matmul(
+                    back[:, t, :],
+                    src[:, i, :],
+                    ident[:],
+                    start=(first and i == 0),
+                    stop=(last and i == len(planes) - 1),
+                    is_transpose=True,
+                )
+
+        def finish(back, xc):
+            y = keep.tile([P, PACK, P], F32, name="y%d" % xc)
+            y_bf = keep.tile([P, P, PACK], BF16, name="y_bf%d" % xc, align_bytes=64)
             nc.scalar.copy(out=y_bf[:], in_=back[:].rearrange("p t x -> p x t"))
-            nc.scalar.copy(out=y[:, :, P * c : P * (c + 1)], in_=back[:])
-            quantise(y_bf, P * c)
-        nc.sync.dma_start(out=out_rows[:, :, 0:WIDE], in_=y[:])
-        nc.sync.dma_start(out=out_words[:, 0:WIDE], in_=y_codes[:, 0:WIDE].bitcast(I32))
+            nc.scalar.copy(out=y[:], in_=back[:])
+            nc.sync.dma_start(out=out_rows[:, :, xc : xc + P], in_=y[:])
+            quantise(y_bf, xc)
 
+        def flush(keep_back):
+            while len(later) > keep_back:
+                later.pop(0)()
+
+        planes = range(PACK)
+        x0 = 0
+        for width in GROUPS:
+            chunks = width // P
+            n_turned = 3 if x0 + width == X else 4
+            backs = [psum.tile([P, PACK, P], F32, name="back%d" % ((x0 // P + c) % BACK_BANKS)) for c in range(chunks)]
+            for j in range(n_turned):
+                turned = [turn_bank(PACK) for c in range(chunks)]
+                for t in planes:
+                    got = gather(t, j, x0, width)
+                    for c in range(chunks):
+                        nc.tensor.transpose(turned[c][:, t, :], got[:, P * c : P * (c + 1)], ident[:])
+                flush(LAG)
+                for c in range(chunks):
+                    col = 4 * j + x0 // P + c
+                    weighted = keep.tile([P, PACK, P], F32, name="weighted%d_%d_%d" % (x0, c, j))
+                    nc.scalar.activation(weighted[:], turned[c][:], COPY, scale=w_cols[:, col : col + 1])
+
+                    def rest(c=c, j=j, weighted=weighted, backs=backs, x0=x0, n_turned=n_turned):
+                        turn_back(backs[c], weighted, planes, j == 0, j == n_turned - 1)
+                        if j == 3:
+                            finish(backs[c], x0 + P * c)
+
+                    later.append(rest)
+            x0 = x0 + width
+        flush(0)
+        x0 = X - LAST
+        prod = keep.tile([P, PACK, LAST], F32, name="ring%d" % (len(gathered) % RING))
+        for t in planes:
+            nc.vector.tensor_tensor(prod[:, t, :], listed(t, 3, x0, LAST), w3_last[:], MULT)
         y = keep.tile([P, PACK, LAST], F32, name="y_last")
-        for t in range(PACK - 1):
-            turned_t = psum.tile([P, P], F32, name="work")
-            for j in range(4):
-                add_turned(turned_t[:], product(t, j, WIDE, LAST)[:], j)
-            y_turned = keep.tile([P, P], F32, name="y_turned_last%d" % t)
-            nc.scalar.copy(out=y_turned[:], in_=turned_t[:])
-            back = psum.tile([P, P], F32, name="back")
-            nc.tensor.transpose(back[:], y_turned[:], ident[:])
-            nc.scalar.copy(out=y[:, t, :], in_=back[:])
-        nc.scalar.dma_start(out=out_rows[:, 0 : PACK - 1, WIDE:X], in_=y[:, 0 : PACK - 1, :])
-        t = PACK - 1
-        p0 = product(t, 0, WIDE, LAST)
-        p1 = product(t, 1, WIDE, LAST)
-        p2 = product(t, 2, WIDE, LAST)
-        nc.vector.tensor_tensor(p0[:], p0[:], p1[:], ADD)
-        p3 = product(t, 3, WIDE, LAST)
-        nc.vector.tensor_tensor(p0[:], p0[:], p2[:], ADD)
-        nc.vector.tensor_tensor(y[:, t, :], p0[:], p3[:], ADD)
-        nc.sync.dma_start(out=out_rows[:, t, WIDE:X], in_=y[:, t, :])
-        y_bf = keep.tile([P, P, PACK], BF16, name="y_bf_last", align_bytes=64)
+        nc.vector.tensor_tensor(y[:], backs[0][:], prod[:], ADD)
+        nc.scalar.dma_start(out=out_rows[:, :, x0:X], in_=y[:])
+        y_bf = keep.tile([P, LAST, PACK], BF16, name="y_bf_last", align_bytes=64)
         nc.vector.tensor_copy(out=y_bf[:], in_=y[:].rearrange("p t x -> p x t"))
-        quantise(y_bf, WIDE)
-        nc.sync.dma_start(out=out_words[:, WIDE:X], in_=y_codes[:, WIDE:X].bitcast(I32))
+        quantise(y_bf, x0)
         for q in range(4):
             queue = nc.sync if q % 2 == 0 else nc.scalar
             queue.dma_start(

@@ -17,18 +17,13 @@ E4M3 = mybir.dt.float8_e4m3fn_x4
 E2M1 = mybir.dt.float4_e2m1fn_x4
 MULT = mybir.AluOpType.mult
 ADD = mybir.AluOpType.add
-COPY = mybir.ActivationFunctionType.Copy
 
 P = 128
 PACK = 4
 N = 512
 DY_CHUNKS = (256, 256, 256, 256)
-GROUPS = (256, 128, 128)
-LAST = GROUPS[-1]
-RING = 6
-TURN_BANKS = 3
-BACK_BANKS = 4
-LAG = 0
+WIDE = 384
+LAST = X - WIDE
 
 
 def tile_attend_gupsamp_pl_kernel(
@@ -63,11 +58,7 @@ def tile_attend_gupsamp_pl_kernel(
                     )
         for j, f in enumerate((f0offs, f1offs, f2offs, f3offs)):
             nc.sync.dma_start(offs[j][:], f)
-        w_rows = keep.tile([P, P], F32, name="w_rows")
         make_identity(nc, ident[:])
-        nc.scalar.activation(w_rows[:], ident[:], COPY, scale=0.0)
-        for j, w in enumerate((w0, w1, w2, w3)):
-            nc.sync.dma_start(out=w_rows[4 * j : 4 * j + 4, :], in_=w[0].rearrange("(c x) -> c x", x=P))
 
         nc.vector.tensor_copy(
             out=w_dealt[:].bitcast(U16).rearrange("p (t q) -> p t q", t=PACK),
@@ -92,7 +83,7 @@ def tile_attend_gupsamp_pl_kernel(
             )
         for t in range(PACK):
             for h in range(2):
-                bank = psum.tile([P, N], F32, name=("work%d" % (t % TURN_BANKS) if h else "back%d" % (t % BACK_BANKS)))
+                bank = psum.tile([P, N], F32, name=("turn%d" if h else "back%d") % t)
                 nc.tensor.matmul_mx(
                     out=bank[:],
                     lhsT=w_dealt[:, 2 * P * t : 2 * P * (t + 1)].bitcast(E2M1),
@@ -104,35 +95,45 @@ def tile_attend_gupsamp_pl_kernel(
                 )
                 nc.scalar.copy(out=u[t][:, N * h : N * (h + 1)], in_=bank[:])
 
-        w3_last = keep.tile([P, LAST], F32, name="stage0")
-        nc.sync.dma_start(out=w3_last[:], in_=w3[:, X - LAST : X])
-        w_bank = psum.tile([P, P], F32, name="back%d" % (BACK_BANKS - 1))
-        nc.tensor.transpose(w_bank[:], w_rows[:], ident[:])
-        w_cols = keep.tile([P, 16], F32, name="w_cols")
-        nc.scalar.activation(w_cols[:], w_bank[:, 0:16], COPY)
+        wts = []
+        for k, pair in enumerate(((w0, w1), (w2, w3))):
+            both = keep.tile([P, 2, X], F32, name="stage%d" % k)
+            for e, w in enumerate(pair):
+                nc.sync.dma_start(out=both[:, e, :], in_=w)
+                wts.append(both[:, e, :])
 
         y_codes = keep.tile([P, X], U32, name="y_codes", align_bytes=64)
         y_scales = keep.tile([P, X], U8, name="y_scales", align_bytes=64)
         out_rows = out_0.rearrange("(p t) x -> p t x", t=PACK)
         out_words = out_1[0].rearrange("p x t -> p (x t)").bitcast(I32)
 
-        gathered = []
-        units = []
-        later = []
+        def product(out, t, j, x0, width):
+            nc.vector.tensor_tensor(
+                out,
+                u[t][:].indirect(offs[j][:, x0 // 16 : (x0 + width) // 16]),
+                wts[j][:, x0 : x0 + width],
+                MULT,
+            )
 
-        def listed(t, j, x0, width):
-            return u[t][:].indirect(offs[j][:, x0 // 16 : (x0 + width) // 16])
-
-        def gather(t, j, x0, width):
-            got = keep.tile([P, width], F32, name="ring%d" % (len(gathered) % RING))
-            gathered.append(got)
-            nc.vector.tensor_copy(got[:], listed(t, j, x0, width))
-            return got
-
-        def turn_bank(planes):
-            bank = psum.tile([P, planes, P], F32, name="work%d" % (len(units) % TURN_BANKS))
-            units.append(bank)
-            return bank
+        def plane_sum(t, x0, width, lists, backs, bank):
+            chunks = width // P
+            turned = psum.tile([P, chunks, P], F32, name="turn%d" % bank)
+            for j in range(lists):
+                prod = keep.tile([P, width], F32, name="prod%d_%d_%d" % (x0, t, j))
+                product(prod[:], t, j, x0, width)
+                for c in range(chunks):
+                    nc.tensor.matmul(
+                        turned[:, c, :],
+                        prod[:, P * c : P * (c + 1)],
+                        ident[:],
+                        start=(j == 0 and c == 0),
+                        stop=(j == lists - 1 and c == chunks - 1),
+                        is_transpose=True,
+                    )
+            summed = keep.tile([P, chunks, P], F32, name="summed%d_%d" % (x0, t))
+            nc.scalar.copy(out=summed[:], in_=turned[:])
+            for c in range(chunks):
+                nc.tensor.transpose(backs[c][:, t, :], summed[:, c, :], ident[:])
 
         def quantise(y_bf, xc):
             nc.vector.quantize_mx(
@@ -142,65 +143,36 @@ def tile_attend_gupsamp_pl_kernel(
             )
             nc.sync.dma_start(out=out_words[:, xc : xc + P], in_=y_codes[:, xc : xc + P].bitcast(I32))
 
-        def turn_back(back, src, planes, first, last):
-            for i, t in enumerate(planes):
-                nc.tensor.matmul(
-                    back[:, t, :],
-                    src[:, i, :],
-                    ident[:],
-                    start=(first and i == 0),
-                    stop=(last and i == len(planes) - 1),
-                    is_transpose=True,
-                )
+        backs = [psum.tile([P, PACK, P], F32, name="back%d" % c) for c in range(X // P)]
+        y_wide = keep.tile([P, PACK, WIDE], F32, name="y_wide")
+        def store_plane(t):
+            for c in range(WIDE // P):
+                nc.scalar.copy(out=y_wide[:, t, P * c : P * (c + 1)], in_=backs[c][:, t, :])
+            nc.sync.dma_start(out=out_rows[:, t, 0:WIDE], in_=y_wide[:, t, :])
 
-        def finish(back, xc):
-            y = keep.tile([P, PACK, P], F32, name="y%d" % xc)
-            y_bf = keep.tile([P, P, PACK], BF16, name="y_bf%d" % xc, align_bytes=64)
-            nc.scalar.copy(out=y_bf[:], in_=back[:].rearrange("p t x -> p x t"))
-            nc.scalar.copy(out=y[:], in_=back[:])
-            nc.sync.dma_start(out=out_rows[:, :, xc : xc + P], in_=y[:])
-            quantise(y_bf, xc)
+        def planes_of(c):
+            y_bf = keep.tile([P, P, PACK], BF16, name="y_bf%d" % c, align_bytes=64)
+            nc.scalar.copy(out=y_bf[:], in_=backs[c][:].rearrange("p t x -> p x t"))
+            quantise(y_bf, P * c)
 
-        def flush(keep_back):
-            while len(later) > keep_back:
-                later.pop(0)()
-
-        planes = range(PACK)
-        x0 = 0
-        for width in GROUPS:
-            chunks = width // P
-            n_turned = 3 if x0 + width == X else 4
-            backs = [psum.tile([P, PACK, P], F32, name="back%d" % ((x0 // P + c) % BACK_BANKS)) for c in range(chunks)]
-            for j in range(n_turned):
-                turned = [turn_bank(PACK) for c in range(chunks)]
-                for t in planes:
-                    got = gather(t, j, x0, width)
-                    for c in range(chunks):
-                        nc.tensor.transpose(turned[c][:, t, :], got[:, P * c : P * (c + 1)], ident[:])
-                flush(LAG)
-                for c in range(chunks):
-                    col = 4 * j + x0 // P + c
-                    weighted = keep.tile([P, PACK, P], F32, name="weighted%d_%d_%d" % (x0, c, j))
-                    nc.scalar.activation(weighted[:], turned[c][:], COPY, scale=w_cols[:, col : col + 1])
-
-                    def rest(c=c, j=j, weighted=weighted, backs=backs, x0=x0, n_turned=n_turned):
-                        turn_back(backs[c], weighted, planes, j == 0, j == n_turned - 1)
-                        if j == 3:
-                            finish(backs[c], x0 + P * c)
-
-                    later.append(rest)
-            x0 = x0 + width
-        flush(0)
-        x0 = X - LAST
-        prod = keep.tile([P, PACK, LAST], F32, name="ring%d" % (len(gathered) % RING))
-        for t in planes:
-            nc.vector.tensor_tensor(prod[:, t, :], listed(t, 3, x0, LAST), w3_last[:], MULT)
+        for t in range(PACK):
+            plane_sum(t, 0, WIDE, 4, backs, t)
+            if t < PACK - 1:
+                store_plane(t)
+        for t in range(PACK):
+            plane_sum(t, WIDE, LAST, 3, backs[-1:], (0, 1, 2, 3)[t])
+        store_plane(PACK - 1)
+        for c in range(WIDE // P):
+            planes_of(c)
+        prod = keep.tile([P, PACK, LAST], F32, name="prod_last")
+        for t in range(PACK):
+            product(prod[:, t, :], t, 3, WIDE, LAST)
         y = keep.tile([P, PACK, LAST], F32, name="y_last")
-        nc.vector.tensor_tensor(y[:], backs[0][:], prod[:], ADD)
-        nc.scalar.dma_start(out=out_rows[:, :, x0:X], in_=y[:])
+        nc.vector.tensor_tensor(y[:], backs[-1][:], prod[:], ADD)
+        nc.scalar.dma_start(out=out_rows[:, :, WIDE:X], in_=y[:])
         y_bf = keep.tile([P, LAST, PACK], BF16, name="y_bf_last", align_bytes=64)
         nc.vector.tensor_copy(out=y_bf[:], in_=y[:].rearrange("p t x -> p x t"))
-        quantise(y_bf, x0)
+        quantise(y_bf, WIDE)
         for q in range(4):
             queue = nc.sync if q % 2 == 0 else nc.scalar
             queue.dma_start(

@@ -20,10 +20,16 @@ ADD = mybir.AluOpType.add
 
 P = 128
 PACK = 4
+LISTS = 4
+QUADS = 4
 N = 512
-DY_CHUNKS = (256, 256, 256, 256)
-WIDE = 384
-LAST = X - WIDE
+PER_COLUMN = 16
+
+TAIL = 128
+DY_PIECES = ((256, 128), (256, 64), (256, 64), (TAIL, 0), (TAIL, 0))
+
+LAST = P
+WIDE = X - LAST
 
 
 def tile_attend_gupsamp_pl_kernel(
@@ -34,26 +40,26 @@ def tile_attend_gupsamp_pl_kernel(
         keep = ctx.enter_context(tc.tile_pool(name="keep", bufs=1))
         psum = ctx.enter_context(tc.psum_pool(name="psum", bufs=1))
 
-        offs = [keep.tile([P, X // 16], U16, name="offs%d" % j) for j in range(4)]
-        w_raw = keep.tile([P, 2 * D], U8, name="w_raw", align_bytes=64)
-        ws_raw = keep.tile([P, D], U8, name="ws_raw", align_bytes=64)
-        w_dealt = keep.tile([P, 2 * D], U8, name="w_dealt", align_bytes=64)
-        ws_dealt = keep.tile([P, D], U8, name="ws_dealt", align_bytes=64)
+        offs = [keep.tile([P, X // PER_COLUMN], U16, name="offs%d" % j) for j in range(LISTS)]
+        mat_words = keep.tile([P, 2 * D], U8, name="mat_words", align_bytes=64)
+        mat_scales = keep.tile([P, D], U8, name="mat_scales", align_bytes=64)
+        dealt_words = keep.tile([P, 2 * D], U8, name="dealt_words", align_bytes=64)
+        dealt_scales = keep.tile([P, D], U8, name="dealt_scales", align_bytes=64)
         ident = keep.tile([P, P], F32, name="ident")
 
-        nc.gpsimd.memset(ws_raw[:].bitcast(I32), 0)
-        nc.scalar.dma_start(out=w_raw[:].bitcast(I32), in_=W_words[0].bitcast(I32))
-        raws = []
+        nc.gpsimd.memset(mat_scales[:].bitcast(I32), 0)
+        nc.scalar.dma_start(out=mat_words[:].bitcast(I32), in_=W_words[0].bitcast(I32))
+        pieces = []
         s0 = 0
-        for k, width in enumerate(DY_CHUNKS):
+        for k, (width, on_scalar) in enumerate(DY_PIECES):
             raw = keep.tile([P, PACK, width], F32, name="stage%d" % k)
             nc.sync.dma_start(out=raw[:], in_=dyT[:, s0 : s0 + width].rearrange("(p j) w -> p j w", j=PACK))
-            raws.append((raw, s0, width))
+            pieces.append((raw, s0, width, width - on_scalar))
             s0 = s0 + width
             if k == 0:
-                for q in range(4):
+                for q in range(QUADS):
                     nc.sync.dma_start(
-                        out=ws_raw[32 * q : 32 * q + 4, :].bitcast(I32),
+                        out=mat_scales[32 * q : 32 * q + 4, :].bitcast(I32),
                         in_=W_scales[0, 4 * q : 4 * q + 4, :].bitcast(I32),
                     )
         for j, f in enumerate((f0offs, f1offs, f2offs, f3offs)):
@@ -61,63 +67,74 @@ def tile_attend_gupsamp_pl_kernel(
         make_identity(nc, ident[:])
 
         nc.vector.tensor_copy(
-            out=w_dealt[:].bitcast(U16).rearrange("p (t q) -> p t q", t=PACK),
-            in_=w_raw[:].bitcast(U16).rearrange("p (q t) -> p t q", t=PACK),
+            out=dealt_words[:].bitcast(U16).rearrange("p (t q) -> p t q", t=PACK),
+            in_=mat_words[:].bitcast(U16).rearrange("p (q t) -> p t q", t=PACK),
         )
         nc.vector.tensor_copy(
-            out=ws_dealt[:].rearrange("p (t q) -> p t q", t=PACK),
-            in_=ws_raw[:].rearrange("p (q t) -> p t q", t=PACK),
+            out=dealt_scales[:].rearrange("p (t q) -> p t q", t=PACK),
+            in_=mat_scales[:].rearrange("p (q t) -> p t q", t=PACK),
         )
 
-        codes = [keep.tile([P, N], U32, name="dy_codes%d" % h, align_bytes=64) for h in range(2)]
-        scales = [keep.tile([P, N], U8, name="dy_scales%d" % h, align_bytes=64) for h in range(2)]
+        dy_codes = keep.tile([P, S], U32, name="dy_codes", align_bytes=64)
+        dy_scales = keep.tile([P, S], U8, name="dy_scales", align_bytes=64)
         u = [keep.tile([P, S], F32, name="u%d" % t) for t in range(PACK)]
-        for k, (raw, s0, width) in enumerate(raws):
-            grouped = keep.tile([P, width, PACK], BF16, name="dy_bf%d" % k, align_bytes=64)
-            nc.vector.tensor_copy(out=grouped[:], in_=raw[:].rearrange("p j w -> p w j"))
-            h, c0 = divmod(s0, N)
+        for k, (raw, s0, width, cut) in enumerate(pieces):
+            dy_bf = keep.tile([P, width, PACK], BF16, name="dy_bf%d" % k, align_bytes=64)
+            nc.vector.tensor_copy(out=dy_bf[:, 0:cut, :], in_=raw[:, :, 0:cut].rearrange("p j w -> p w j"))
+            if cut < width:
+                nc.scalar.copy(out=dy_bf[:, cut:width, :], in_=raw[:, :, cut:width].rearrange("p j w -> p w j"))
             nc.vector.quantize_mx(
-                out=codes[h][:, c0 : c0 + width].bitcast(E5M2),
-                scales=scales[h][:, c0 : c0 + width],
-                in_=grouped[:].rearrange("p w j -> p (w j)"),
+                out=dy_codes[:, s0 : s0 + width].bitcast(E5M2),
+                scales=dy_scales[:, s0 : s0 + width],
+                in_=dy_bf[:].rearrange("p w j -> p (w j)"),
             )
-        for t in range(PACK):
-            for h in range(2):
-                bank = psum.tile([P, N], F32, name=("turn%d" if h else "back%d") % t)
-                nc.tensor.matmul_mx(
-                    out=bank[:],
-                    lhsT=w_dealt[:, 2 * P * t : 2 * P * (t + 1)].bitcast(E2M1),
-                    lhsT_scale=ws_dealt[:, P * t : P * (t + 1)],
-                    rhs=codes[h][:].bitcast(E5M2),
-                    rhs_scale=scales[h][:],
-                    start=True,
-                    stop=True,
-                )
-                nc.scalar.copy(out=u[t][:, N * h : N * (h + 1)], in_=bank[:])
 
-        wts = []
+        def mx_pass(t, first, keep_from, bank_name):
+            bank = psum.tile([P, N], F32, name=bank_name)
+            nc.tensor.matmul_mx(
+                out=bank[:],
+                lhsT=dealt_words[:, 2 * P * t : 2 * P * (t + 1)].bitcast(E2M1),
+                lhsT_scale=dealt_scales[:, P * t : P * (t + 1)],
+                rhs=dy_codes[:, first : first + N].bitcast(E5M2),
+                rhs_scale=dy_scales[:, first : first + N],
+                start=True,
+                stop=True,
+            )
+            nc.scalar.copy(out=u[t][:, keep_from : first + N], in_=bank[:, keep_from - first : N])
+
+        mx_pass(0, 0, 0, "back0")
+        mx_pass(1, 0, 0, "back2")
+        mx_pass(0, N - TAIL, N, "back1")
+        mx_pass(0, N, S - TAIL, "turn0")
+        mx_pass(1, N, N, "turn1")
+        mx_pass(2, 0, 0, "back1")
+        mx_pass(2, N, N, "turn2")
+        mx_pass(3, 0, 0, "back3")
+        mx_pass(3, N, N, "turn3")
+
+        weights = []
         for k, pair in enumerate(((w0, w1), (w2, w3))):
-            both = keep.tile([P, 2, X], F32, name="stage%d" % k)
+            both = keep.tile([P, len(pair), X], F32, name="stage%d" % k)
             for e, w in enumerate(pair):
                 nc.sync.dma_start(out=both[:, e, :], in_=w)
-                wts.append(both[:, e, :])
+                weights.append(both[:, e, :])
 
         y_codes = keep.tile([P, X], U32, name="y_codes", align_bytes=64)
         y_scales = keep.tile([P, X], U8, name="y_scales", align_bytes=64)
-        out_rows = out_0.rearrange("(p t) x -> p t x", t=PACK)
+        out_planes = out_0.rearrange("(p t) x -> p t x", t=PACK)
         out_words = out_1[0].rearrange("p x t -> p (x t)").bitcast(I32)
 
         def product(out, t, j, x0, width):
             nc.vector.tensor_tensor(
                 out,
-                u[t][:].indirect(offs[j][:, x0 // 16 : (x0 + width) // 16]),
-                wts[j][:, x0 : x0 + width],
+                u[t][:].indirect(offs[j][:, x0 // PER_COLUMN : (x0 + width) // PER_COLUMN]),
+                weights[j][:, x0 : x0 + width],
                 MULT,
             )
 
-        def plane_sum(t, x0, width, lists, backs, bank):
+        def plane_sum(t, x0, width, lists, banks):
             chunks = width // P
-            turned = psum.tile([P, chunks, P], F32, name="turn%d" % bank)
+            turned = psum.tile([P, chunks, P], F32, name="turn%d" % t)
             for j in range(lists):
                 prod = keep.tile([P, width], F32, name="prod%d_%d_%d" % (x0, t, j))
                 product(prod[:], t, j, x0, width)
@@ -133,47 +150,47 @@ def tile_attend_gupsamp_pl_kernel(
             summed = keep.tile([P, chunks, P], F32, name="summed%d_%d" % (x0, t))
             nc.scalar.copy(out=summed[:], in_=turned[:])
             for c in range(chunks):
-                nc.tensor.transpose(backs[c][:, t, :], summed[:, c, :], ident[:])
+                nc.tensor.transpose(banks[c][:, t, :], summed[:, c, :], ident[:])
 
-        def quantise(y_bf, xc):
+        def quantise(y_bf, x0):
             nc.vector.quantize_mx(
-                out=y_codes[:, xc : xc + P].bitcast(E4M3),
-                scales=y_scales[:, xc : xc + P],
+                out=y_codes[:, x0 : x0 + P].bitcast(E4M3),
+                scales=y_scales[:, x0 : x0 + P],
                 in_=y_bf[:].rearrange("p x t -> p (x t)"),
             )
-            nc.sync.dma_start(out=out_words[:, xc : xc + P], in_=y_codes[:, xc : xc + P].bitcast(I32))
+            nc.sync.dma_start(out=out_words[:, x0 : x0 + P], in_=y_codes[:, x0 : x0 + P].bitcast(I32))
 
         backs = [psum.tile([P, PACK, P], F32, name="back%d" % c) for c in range(X // P)]
         y_wide = keep.tile([P, PACK, WIDE], F32, name="y_wide")
-        def store_plane(t):
+
+        def store_wide_plane(t):
             for c in range(WIDE // P):
                 nc.scalar.copy(out=y_wide[:, t, P * c : P * (c + 1)], in_=backs[c][:, t, :])
-            nc.sync.dma_start(out=out_rows[:, t, 0:WIDE], in_=y_wide[:, t, :])
+            nc.sync.dma_start(out=out_planes[:, t, 0:WIDE], in_=y_wide[:, t, :])
 
-        def planes_of(c):
+        for t in range(PACK):
+            plane_sum(t, 0, WIDE, LISTS, backs)
+            if t < PACK - 1:
+                store_wide_plane(t)
+        for t in range(PACK):
+            plane_sum(t, WIDE, LAST, LISTS - 1, backs[-1:])
+        store_wide_plane(PACK - 1)
+        for c in range(WIDE // P):
             y_bf = keep.tile([P, P, PACK], BF16, name="y_bf%d" % c, align_bytes=64)
             nc.scalar.copy(out=y_bf[:], in_=backs[c][:].rearrange("p t x -> p x t"))
             quantise(y_bf, P * c)
 
+        prod_last = keep.tile([P, PACK, LAST], F32, name="prod_last")
         for t in range(PACK):
-            plane_sum(t, 0, WIDE, 4, backs, t)
-            if t < PACK - 1:
-                store_plane(t)
-        for t in range(PACK):
-            plane_sum(t, WIDE, LAST, 3, backs[-1:], (0, 1, 2, 3)[t])
-        store_plane(PACK - 1)
-        for c in range(WIDE // P):
-            planes_of(c)
-        prod = keep.tile([P, PACK, LAST], F32, name="prod_last")
-        for t in range(PACK):
-            product(prod[:, t, :], t, 3, WIDE, LAST)
-        y = keep.tile([P, PACK, LAST], F32, name="y_last")
-        nc.vector.tensor_tensor(y[:], backs[-1][:], prod[:], ADD)
-        nc.scalar.dma_start(out=out_rows[:, :, WIDE:X], in_=y[:])
-        y_bf = keep.tile([P, LAST, PACK], BF16, name="y_bf_last", align_bytes=64)
-        nc.vector.tensor_copy(out=y_bf[:], in_=y[:].rearrange("p t x -> p x t"))
-        quantise(y_bf, WIDE)
-        for q in range(4):
+            product(prod_last[:, t, :], t, LISTS - 1, WIDE, LAST)
+        y_last = keep.tile([P, PACK, LAST], F32, name="y_last")
+        nc.vector.tensor_tensor(y_last[:], backs[-1][:], prod_last[:], ADD)
+        nc.scalar.dma_start(out=out_planes[:, :, WIDE:X], in_=y_last[:])
+        y_bf_last = keep.tile([P, LAST, PACK], BF16, name="y_bf_last", align_bytes=64)
+        nc.vector.tensor_copy(out=y_bf_last[:], in_=y_last[:].rearrange("p t x -> p x t"))
+        quantise(y_bf_last, WIDE)
+
+        for q in range(QUADS):
             queue = nc.sync if q % 2 == 0 else nc.scalar
             queue.dma_start(
                 out=out_2[0, 4 * q : 4 * q + 4, :].bitcast(I32),

@@ -26,7 +26,8 @@ N = 512
 PER_COLUMN = 16
 
 TAIL = 128
-DY_PIECES = ((256, 128), (256, 64), (256, 64), (TAIL, 0), (TAIL, 0))
+DY_PIECES = ((256, 96), (256, 96), (256, 112), (TAIL, 64), (TAIL, 48))
+RUN = 4
 
 LAST = P
 WIDE = X - LAST
@@ -48,7 +49,7 @@ def tile_attend_gupsamp_pl_kernel(
         ident = keep.tile([P, P], F32, name="ident")
 
         nc.gpsimd.memset(mat_scales[:].bitcast(I32), 0)
-        nc.scalar.dma_start(out=mat_words[:].bitcast(I32), in_=W_words[0].bitcast(I32))
+        nc.sync.dma_start(out=mat_words[:].bitcast(I32), in_=W_words[0].bitcast(I32))
         pieces = []
         s0 = 0
         for k, (width, on_scalar) in enumerate(DY_PIECES):
@@ -77,19 +78,24 @@ def tile_attend_gupsamp_pl_kernel(
 
         dy_codes = keep.tile([P, S], U32, name="dy_codes", align_bytes=64)
         dy_scales = keep.tile([P, S], U8, name="dy_scales", align_bytes=64)
-        u = [keep.tile([P, S], F32, name="u%d" % t) for t in range(PACK)]
         for k, (raw, s0, width, cut) in enumerate(pieces):
             dy_bf = keep.tile([P, width, PACK], BF16, name="dy_bf%d" % k, align_bytes=64)
-            nc.vector.tensor_copy(out=dy_bf[:, 0:cut, :], in_=raw[:, :, 0:cut].rearrange("p j w -> p w j"))
-            if cut < width:
-                nc.scalar.copy(out=dy_bf[:, cut:width, :], in_=raw[:, :, cut:width].rearrange("p j w -> p w j"))
+            for copy, a, b in ((nc.vector.tensor_copy, 0, cut), (nc.scalar.copy, cut, width)):
+                copy(
+                    out=dy_bf[:, a:b, :].rearrange("p (c i) j -> p c j i", i=RUN),
+                    in_=raw[:, :, a:b].rearrange("p j (c i) -> p c j i", i=RUN),
+                )
             nc.vector.quantize_mx(
                 out=dy_codes[:, s0 : s0 + width].bitcast(E5M2),
                 scales=dy_scales[:, s0 : s0 + width],
                 in_=dy_bf[:].rearrange("p w j -> p (w j)"),
             )
 
-        def mx_pass(t, first, keep_from, bank_name):
+        last = len(pieces) - 1
+        u = [keep.tile([P, S], F32, name="stage%d" % last), keep.tile([P, S], F32, name="dy_bf%d" % last, align_bytes=64)]
+        u.extend(keep.tile([P, S], F32, name="u%d" % t) for t in range(2, PACK))
+
+        def mx_pass(t, first, keep_from, bank_name, copy):
             bank = psum.tile([P, N], F32, name=bank_name)
             nc.tensor.matmul_mx(
                 out=bank[:],
@@ -100,17 +106,17 @@ def tile_attend_gupsamp_pl_kernel(
                 start=True,
                 stop=True,
             )
-            nc.scalar.copy(out=u[t][:, keep_from : first + N], in_=bank[:, keep_from - first : N])
+            copy(out=u[t][:, keep_from : first + N], in_=bank[:, keep_from - first : N])
 
-        mx_pass(0, 0, 0, "back0")
-        mx_pass(1, 0, 0, "back2")
-        mx_pass(0, N - TAIL, N, "back1")
-        mx_pass(0, N, S - TAIL, "turn0")
-        mx_pass(1, N, N, "turn1")
-        mx_pass(2, 0, 0, "back1")
-        mx_pass(2, N, N, "turn2")
-        mx_pass(3, 0, 0, "back3")
-        mx_pass(3, N, N, "turn3")
+        mx_pass(0, 0, 0, "turn0", nc.scalar.copy)
+        mx_pass(0, N - 2 * TAIL, N, "back2", nc.vector.tensor_copy)
+        mx_pass(0, N, S - 2 * TAIL, "back3", nc.vector.tensor_copy)
+        mx_pass(1, 0, 0, "back1", nc.scalar.copy)
+        mx_pass(1, N, N, "turn1", nc.scalar.copy)
+        mx_pass(2, 0, 0, "back3", nc.scalar.copy)
+        mx_pass(2, N, N, "turn2", nc.scalar.copy)
+        mx_pass(3, 0, 0, "turn1", nc.scalar.copy)
+        mx_pass(3, N, N, "turn3", nc.scalar.copy)
 
         weights = []
         for k, pair in enumerate(((w0, w1), (w2, w3))):

@@ -110,7 +110,7 @@ def tile_attend_gupsamp_pl_kernel(
 
         mx_pass(0, 0, 0, "turn0", nc.scalar.copy)
         mx_pass(0, N - 2 * TAIL, N, "back2", nc.vector.tensor_copy)
-        mx_pass(0, N, S - 2 * TAIL, "back3", nc.vector.tensor_copy)
+        mx_pass(0, N, S - 2 * TAIL, "back3", nc.scalar.copy)
         mx_pass(1, 0, 0, "back1", nc.scalar.copy)
         mx_pass(1, N, N, "turn1", nc.scalar.copy)
         mx_pass(2, 0, 0, "back3", nc.scalar.copy)
@@ -125,8 +125,6 @@ def tile_attend_gupsamp_pl_kernel(
                 nc.sync.dma_start(out=both[:, e, :], in_=w)
                 weights.append(both[:, e, :])
 
-        y_codes = keep.tile([P, X], U32, name="y_codes", align_bytes=64)
-        y_scales = keep.tile([P, X], U8, name="y_scales", align_bytes=64)
         out_planes = out_0.rearrange("(p t) x -> p t x", t=PACK)
         out_words = out_1[0].rearrange("p x t -> p (x t)").bitcast(I32)
 
@@ -158,14 +156,6 @@ def tile_attend_gupsamp_pl_kernel(
             for c in range(chunks):
                 nc.tensor.transpose(banks[c][:, t, :], summed[:, c, :], ident[:])
 
-        def quantise(y_bf, x0):
-            nc.vector.quantize_mx(
-                out=y_codes[:, x0 : x0 + P].bitcast(E4M3),
-                scales=y_scales[:, x0 : x0 + P],
-                in_=y_bf[:].rearrange("p x t -> p (x t)"),
-            )
-            nc.sync.dma_start(out=out_words[:, x0 : x0 + P], in_=y_codes[:, x0 : x0 + P].bitcast(I32))
-
         backs = [psum.tile([P, PACK, P], F32, name="back%d" % c) for c in range(X // P)]
         y_wide = keep.tile([P, PACK, WIDE], F32, name="y_wide")
 
@@ -178,23 +168,46 @@ def tile_attend_gupsamp_pl_kernel(
             plane_sum(t, 0, WIDE, LISTS, backs)
             if t < PACK - 1:
                 store_wide_plane(t)
-        for t in range(PACK):
+        for t in range(PACK - 1):
             plane_sum(t, WIDE, LAST, LISTS - 1, backs[-1:])
+        back_end = psum.tile([P, PACK, P], F32, name="turn0")
+        plane_sum(PACK - 1, WIDE, LAST, LISTS - 1, [back_end])
         store_wide_plane(PACK - 1)
+        y_bf = keep.tile([P, WIDE, PACK], BF16, name="y_bf", align_bytes=64)
         for c in range(WIDE // P):
-            y_bf = keep.tile([P, P, PACK], BF16, name="y_bf%d" % c, align_bytes=64)
-            nc.scalar.copy(out=y_bf[:], in_=backs[c][:].rearrange("p t x -> p x t"))
-            quantise(y_bf, P * c)
+            nc.scalar.copy(out=y_bf[:, P * c : P * (c + 1), :], in_=backs[c][:].rearrange("p t x -> p x t"))
 
-        prod_last = keep.tile([P, PACK, LAST], F32, name="prod_last")
-        for t in range(PACK):
-            product(prod_last[:, t, :], t, LISTS - 1, WIDE, LAST)
+        prod_first = keep.tile([P, PACK - 1, LAST], F32, name="prod_first", align_bytes=64)
+        prod_end = keep.tile([P, LAST], F32, name="prod_end")
+        for t in range(PACK - 1):
+            product(prod_first[:, t, :], t, LISTS - 1, WIDE, LAST)
+        product(prod_end[:], PACK - 1, LISTS - 1, WIDE, LAST)
         y_last = keep.tile([P, PACK, LAST], F32, name="y_last")
-        nc.vector.tensor_tensor(y_last[:], backs[-1][:], prod_last[:], ADD)
-        nc.scalar.dma_start(out=out_planes[:, :, WIDE:X], in_=y_last[:])
+        nc.vector.tensor_tensor(y_last[:, 0 : PACK - 1, :], backs[-1][:, 0 : PACK - 1, :], prod_first[:], ADD)
+        nc.vector.tensor_tensor(y_last[:, PACK - 1, :], back_end[:, PACK - 1, :], prod_end[:], ADD)
         y_bf_last = keep.tile([P, LAST, PACK], BF16, name="y_bf_last", align_bytes=64)
-        nc.vector.tensor_copy(out=y_bf_last[:], in_=y_last[:].rearrange("p t x -> p x t"))
-        quantise(y_bf_last, WIDE)
+        for copy, a, b in ((nc.scalar.copy, 0, LAST // 2), (nc.vector.tensor_copy, LAST // 2, LAST)):
+            copy(
+                out=y_bf_last[:, a:b, :].rearrange("p (c i) t -> p c t i", i=RUN),
+                in_=y_last[:, :, a:b].rearrange("p t (c i) -> p c t i", i=RUN),
+            )
+        nc.sync.dma_start(out=out_planes[:, :, WIDE:X], in_=y_last[:])
+
+        y_codes = keep.tile([P, X], U32, name="prod_first", align_bytes=64)
+        y_scales = keep.tile([P, X], U8, name="y_scales", align_bytes=64)
+
+        def quantise(rounded, x0, width):
+            nc.vector.quantize_mx(
+                out=y_codes[:, x0 : x0 + width].bitcast(E4M3),
+                scales=y_scales[:, x0 : x0 + width],
+                in_=rounded.rearrange("p x t -> p (x t)"),
+            )
+
+        quantise(y_bf[:, 0 : 2 * P, :], 0, 2 * P)
+        quantise(y_bf[:, 2 * P : WIDE, :], 2 * P, P)
+        nc.sync.dma_start(out=out_words[:, 0:WIDE], in_=y_codes[:, 0:WIDE].bitcast(I32))
+        quantise(y_bf_last[:], WIDE, LAST)
+        nc.sync.dma_start(out=out_words[:, WIDE:X], in_=y_codes[:, WIDE:X].bitcast(I32))
 
         for q in range(QUADS):
             queue = nc.sync if q % 2 == 0 else nc.scalar

@@ -177,21 +177,14 @@ def tile_attend_gupsamp_pl_kernel(
         for c in range(WIDE // P):
             nc.scalar.copy(out=y_bf[:, P * c : P * (c + 1), :], in_=backs[c][:].rearrange("p t x -> p x t"))
 
-        prod_first = keep.tile([P, PACK - 1, LAST], F32, name="prod_first", align_bytes=64)
-        prod_end = keep.tile([P, LAST], F32, name="prod_end")
-        for t in range(PACK - 1):
-            product(prod_first[:, t, :], t, LISTS - 1, WIDE, LAST)
-        product(prod_end[:], PACK - 1, LISTS - 1, WIDE, LAST)
+        prod_first = keep.tile([P, 1, LAST], F32, name="prod_first", align_bytes=64)
+        prod_end = keep.tile([P, PACK - 1, LAST], F32, name="prod_end")
+        for t in range(PACK):
+            product(prod_first[:, 0, :] if t == 0 else prod_end[:, t - 1, :], t, LISTS - 1, WIDE, LAST)
         y_last = keep.tile([P, PACK, LAST], F32, name="y_last")
-        nc.vector.tensor_tensor(y_last[:, 0 : PACK - 1, :], backs[-1][:, 0 : PACK - 1, :], prod_first[:], ADD)
-        nc.vector.tensor_tensor(y_last[:, PACK - 1, :], back_end[:, PACK - 1, :], prod_end[:], ADD)
-        y_bf_last = keep.tile([P, LAST, PACK], BF16, name="y_bf_last", align_bytes=64)
-        for copy, a, b in ((nc.scalar.copy, 0, LAST // 2), (nc.vector.tensor_copy, LAST // 2, LAST)):
-            copy(
-                out=y_bf_last[:, a:b, :].rearrange("p (c i) t -> p c t i", i=RUN),
-                in_=y_last[:, :, a:b].rearrange("p t (c i) -> p c t i", i=RUN),
-            )
-        nc.sync.dma_start(out=out_planes[:, :, WIDE:X], in_=y_last[:])
+        nc.vector.tensor_tensor(y_last[:, 0, :], backs[-1][:, 0, :], prod_first[:, 0, :], ADD)
+        nc.vector.tensor_tensor(y_last[:, 1:3, :], backs[-1][:, 1:3, :], prod_end[:, 0:2, :], ADD)
+        nc.sync.dma_start(out=out_planes[:, 0 : PACK - 1, WIDE:X], in_=y_last[:, 0 : PACK - 1, :])
 
         y_codes = keep.tile([P, X], U32, name="prod_first", align_bytes=64)
         y_scales = keep.tile([P, X], U8, name="y_scales", align_bytes=64)
@@ -204,8 +197,16 @@ def tile_attend_gupsamp_pl_kernel(
             )
 
         quantise(y_bf[:, 0 : 2 * P, :], 0, 2 * P)
+        nc.vector.tensor_tensor(y_last[:, PACK - 1, :], back_end[:, PACK - 1, :], prod_end[:, 2, :], ADD)
+        nc.sync.dma_start(out=out_planes[:, PACK - 1, WIDE:X], in_=y_last[:, PACK - 1, :])
         quantise(y_bf[:, 2 * P : WIDE, :], 2 * P, P)
         nc.sync.dma_start(out=out_words[:, 0:WIDE], in_=y_codes[:, 0:WIDE].bitcast(I32))
+        y_bf_last = keep.tile([P, LAST, PACK], BF16, name="y_bf_last", align_bytes=64)
+        for copy, a, b in ((nc.scalar.copy, 0, LAST // 2), (nc.vector.tensor_copy, LAST // 2, LAST)):
+            copy(
+                out=y_bf_last[:, a:b, :].rearrange("p (c i) t -> p c t i", i=RUN),
+                in_=y_last[:, :, a:b].rearrange("p t (c i) -> p c t i", i=RUN),
+            )
         quantise(y_bf_last[:], WIDE, LAST)
         nc.sync.dma_start(out=out_words[:, WIDE:X], in_=y_codes[:, WIDE:X].bitcast(I32))
 

@@ -26,7 +26,7 @@ N = 512
 PER_COLUMN = 16
 
 TAIL = 128
-DY_PIECES = ((256, 96), (256, 96), (256, 112), (TAIL, 64), (TAIL, 48))
+DY_PIECES = ((256, 112), (256, 112), (256, 112), (TAIL, 64), (TAIL, 64))
 RUN = 4
 
 LAST = P
@@ -71,10 +71,12 @@ def tile_attend_gupsamp_pl_kernel(
             out=dealt_words[:].bitcast(U16).rearrange("p (t q) -> p t q", t=PACK),
             in_=mat_words[:].bitcast(U16).rearrange("p (q t) -> p t q", t=PACK),
         )
-        nc.vector.tensor_copy(
-            out=dealt_scales[:].rearrange("p (t q) -> p t q", t=PACK),
-            in_=mat_scales[:].rearrange("p (q t) -> p t q", t=PACK),
-        )
+
+        def deal_scales(t):
+            nc.vector.tensor_copy(
+                out=dealt_scales[:, P * t : P * (t + 1)],
+                in_=mat_scales[:].rearrange("p (q t) -> p t q", t=PACK)[:, t, :],
+            )
 
         dy_codes = keep.tile([P, S], U32, name="dy_codes", align_bytes=64)
         dy_scales = keep.tile([P, S], U8, name="dy_scales", align_bytes=64)
@@ -90,6 +92,11 @@ def tile_attend_gupsamp_pl_kernel(
                 scales=dy_scales[:, s0 : s0 + width],
                 in_=dy_bf[:].rearrange("p w j -> p (w j)"),
             )
+            if k == 0:
+                deal_scales(0)
+                deal_scales(1)
+        deal_scales(2)
+        deal_scales(3)
 
         last = len(pieces) - 1
         u = [keep.tile([P, S], F32, name="stage%d" % last), keep.tile([P, S], F32, name="dy_bf%d" % last, align_bytes=64)]

@@ -98,11 +98,9 @@ def tile_attend_gupsamp_pl_kernel(
         deal_scales(2)
         deal_scales(3)
 
-        last = len(pieces) - 1
-        u = [keep.tile([P, S], F32, name="stage%d" % last), keep.tile([P, S], F32, name="dy_bf%d" % last, align_bytes=64)]
-        u.extend(keep.tile([P, S], F32, name="u%d" % t) for t in range(2, PACK))
+        u = [keep.tile([P, S], F32, name="stage%d" % (len(pieces) - 1))]
 
-        def mx_pass(t, first, keep_from, bank_name, copy):
+        def mx_pass(t, first, bank_name):
             bank = psum.tile([P, N], F32, name=bank_name)
             nc.tensor.matmul_mx(
                 out=bank[:],
@@ -113,17 +111,22 @@ def tile_attend_gupsamp_pl_kernel(
                 start=True,
                 stop=True,
             )
-            copy(out=u[t][:, keep_from : first + N], in_=bank[:, keep_from - first : N])
+            return bank
 
-        mx_pass(0, 0, 0, "turn0", nc.scalar.copy)
-        mx_pass(0, N - 2 * TAIL, N, "back2", nc.vector.tensor_copy)
-        mx_pass(0, N, S - 2 * TAIL, "back3", nc.scalar.copy)
-        mx_pass(1, 0, 0, "back1", nc.scalar.copy)
-        mx_pass(1, N, N, "turn1", nc.scalar.copy)
-        mx_pass(2, 0, 0, "back3", nc.scalar.copy)
-        mx_pass(2, N, N, "turn2", nc.scalar.copy)
-        mx_pass(3, 0, 0, "turn1", nc.scalar.copy)
-        mx_pass(3, N, N, "turn3", nc.scalar.copy)
+        banks = [mx_pass(0, 0, "turn2"), mx_pass(0, N - 2 * TAIL, "turn3"), mx_pass(0, N, "turn1")]
+        nc.scalar.copy(out=u[0][:, 0:N], in_=banks[0][:])
+        nc.vector.tensor_copy(out=u[0][:, N : S - 2 * TAIL], in_=banks[1][:, 2 * TAIL : N])
+        nc.scalar.copy(out=u[0][:, S - 2 * TAIL : S], in_=banks[2][:, N - 2 * TAIL : N])
+        later = {
+            t: [mx_pass(t, N * h, name) for h, name in enumerate(names)]
+            for t, names in ((1, ("back0", "back1")), (2, ("back2", "back3")), (3, ("turn2", "turn3")))
+        }
+
+        def copy_plane(t, name):
+            plane = keep.tile([P, S], F32, name=name)
+            for h, bank in enumerate(later[t]):
+                nc.scalar.copy(out=plane[:, N * h : N * (h + 1)], in_=bank[:])
+            u.append(plane)
 
         weights = []
         for k, pair in enumerate(((w0, w1), (w2, w3))):
@@ -143,57 +146,81 @@ def tile_attend_gupsamp_pl_kernel(
                 MULT,
             )
 
-        def plane_sum(t, x0, width, lists, banks):
-            chunks = width // P
-            turned = psum.tile([P, chunks, P], F32, name="turn%d" % t)
-            for j in range(lists):
-                prod = keep.tile([P, width], F32, name="prod%d_%d_%d" % (x0, t, j))
-                product(prod[:], t, j, x0, width)
-                for c in range(chunks):
+        def plane_sum(t, c0, groups):
+            places = []
+            turned = []
+            for name, count in groups:
+                bank = psum.tile([P, count, P], F32, name=name)
+                turned.append(bank)
+                first = c0 + len(places)
+                final = max((LISTS - 1 if first + c < WIDE // P else LISTS - 2, c) for c in range(count))
+                places.extend((bank, c, final) for c in range(count))
+            for j in range(LISTS):
+                count = len(places) if j < LISTS - 1 else min(len(places), WIDE // P - c0)
+                prod = keep.tile([P, count * P], F32, name="prod%d_%d_%d" % (c0, t, j))
+                product(prod[:], t, j, c0 * P, count * P)
+                for i in range(count):
+                    bank, c, final = places[i]
                     nc.tensor.matmul(
-                        turned[:, c, :],
-                        prod[:, P * c : P * (c + 1)],
+                        bank[:, c, :],
+                        prod[:, P * i : P * (i + 1)],
                         ident[:],
                         start=(j == 0 and c == 0),
-                        stop=(j == lists - 1 and c == chunks - 1),
+                        stop=((j, c) == final),
                         is_transpose=True,
                     )
-            summed = keep.tile([P, chunks, P], F32, name="summed%d_%d" % (x0, t))
+                if t == 0 and j < PACK - 1:
+                    copy_plane(j + 1, "prod0_0_%d" % j)
+            return turned
+
+        def turn_back(t, c0, turned, banks):
+            chunks = turned.shape[1]
+            summed = keep.tile([P, chunks, P], F32, name="summed%d_%d" % (c0, t))
             nc.scalar.copy(out=summed[:], in_=turned[:])
             for c in range(chunks):
-                nc.tensor.transpose(banks[c][:, t, :], summed[:, c, :], ident[:])
+                nc.tensor.transpose(banks[c0 + c][:, t, :], summed[:, c, :], ident[:])
 
         backs = [psum.tile([P, PACK, P], F32, name="back%d" % c) for c in range(X // P)]
-        y_wide = keep.tile([P, PACK, WIDE], F32, name="y_wide")
+        y_wide = keep.tile([P, PACK - 1, WIDE], F32, name="y_wide")
+        y_half = keep.tile([P, 2 * P], F32, name="y_half")
+        y_end = keep.tile([P, PACK, 2 * P], F32, name="y_end")
+        y_last = y_end[:, :, P : 2 * P]
+        y_bf = keep.tile([P, 2 * P, PACK], BF16, name="y_bf", align_bytes=64)
+        y_bf_mid = keep.tile([P, P, PACK], BF16, name="y_bf_mid", align_bytes=64)
 
-        def store_wide_plane(t):
+        def round_chunk(c):
+            rounded = y_bf[:, P * c : P * (c + 1), :] if c < 2 else y_bf_mid[:]
+            nc.scalar.copy(out=rounded, in_=backs[c][:].rearrange("p t x -> p x t"))
+
+        for t in range(PACK - 1):
+            groups = (("turn%d" % t, 4),) if t < 2 else (("turn2", 2), ("turn3", 2))
+            for g, turned in enumerate(plane_sum(t, 0, groups)):
+                turn_back(t, 2 * g, turned, backs)
             for c in range(WIDE // P):
                 nc.scalar.copy(out=y_wide[:, t, P * c : P * (c + 1)], in_=backs[c][:, t, :])
             nc.sync.dma_start(out=out_planes[:, t, 0:WIDE], in_=y_wide[:, t, :])
-
-        for t in range(PACK):
-            plane_sum(t, 0, WIDE, LISTS, backs)
-            if t < PACK - 1:
-                store_wide_plane(t)
-        for t in range(PACK - 1):
-            plane_sum(t, WIDE, LAST, LISTS - 1, backs[-1:])
+        t = PACK - 1
+        for c, turned in enumerate(plane_sum(t, 0, (("turn0", 1), ("turn1", 1)))):
+            turn_back(t, c, turned, backs)
+        turned = plane_sum(t, 2, (("turn2", 1), ("turn3", 1)))
+        for c in range(2):
+            nc.scalar.copy(out=y_half[:, P * c : P * (c + 1)], in_=backs[c][:, t, :])
+        nc.sync.dma_start(out=out_planes[:, t, 0 : 2 * P], in_=y_half[:])
+        round_chunk(0)
         back_end = psum.tile([P, PACK, P], F32, name="turn0")
-        plane_sum(PACK - 1, WIDE, LAST, LISTS - 1, [back_end])
-        store_wide_plane(PACK - 1)
-        y_bf = keep.tile([P, WIDE, PACK], BF16, name="y_bf", align_bytes=64)
-        for c in range(WIDE // P):
-            nc.scalar.copy(out=y_bf[:, P * c : P * (c + 1), :], in_=backs[c][:].rearrange("p t x -> p x t"))
+        turn_back(t, 3, turned[1], backs[:-1] + [back_end])
+        turn_back(t, 2, turned[0], backs)
+        round_chunk(1)
+        nc.scalar.copy(out=y_end[:, t, 0:P], in_=backs[2][:, t, :])
+        round_chunk(2)
 
-        prod_first = keep.tile([P, 1, LAST], F32, name="prod_first", align_bytes=64)
-        prod_end = keep.tile([P, PACK - 1, LAST], F32, name="prod_end")
+        prod_end = keep.tile([P, PACK, LAST], F32, name="summed0_3")
         for t in range(PACK):
-            product(prod_first[:, 0, :] if t == 0 else prod_end[:, t - 1, :], t, LISTS - 1, WIDE, LAST)
-        y_last = keep.tile([P, PACK, LAST], F32, name="y_last")
-        nc.vector.tensor_tensor(y_last[:, 0, :], backs[-1][:, 0, :], prod_first[:, 0, :], ADD)
-        nc.vector.tensor_tensor(y_last[:, 1:3, :], backs[-1][:, 1:3, :], prod_end[:, 0:2, :], ADD)
+            product(prod_end[:, t, :], t, LISTS - 1, WIDE, LAST)
+        nc.vector.tensor_tensor(y_last[:, 0:3, :], backs[-1][:, 0:3, :], prod_end[:, 0:3, :], ADD)
         nc.sync.dma_start(out=out_planes[:, 0 : PACK - 1, WIDE:X], in_=y_last[:, 0 : PACK - 1, :])
 
-        y_codes = keep.tile([P, X], U32, name="prod_first", align_bytes=64)
+        y_codes = keep.tile([P, X], U32, name="y_codes", align_bytes=64)
         y_scales = keep.tile([P, X], U8, name="y_scales", align_bytes=64)
 
         def quantise(rounded, x0, width):
@@ -203,19 +230,18 @@ def tile_attend_gupsamp_pl_kernel(
                 in_=rounded.rearrange("p x t -> p (x t)"),
             )
 
-        quantise(y_bf[:, 0 : 2 * P, :], 0, 2 * P)
-        nc.vector.tensor_tensor(y_last[:, PACK - 1, :], back_end[:, PACK - 1, :], prod_end[:, 2, :], ADD)
-        nc.sync.dma_start(out=out_planes[:, PACK - 1, WIDE:X], in_=y_last[:, PACK - 1, :])
-        quantise(y_bf[:, 2 * P : WIDE, :], 2 * P, P)
-        nc.sync.dma_start(out=out_words[:, 0:WIDE], in_=y_codes[:, 0:WIDE].bitcast(I32))
-        y_bf_last = keep.tile([P, LAST, PACK], BF16, name="y_bf_last", align_bytes=64)
-        for copy, a, b in ((nc.scalar.copy, 0, LAST // 2), (nc.vector.tensor_copy, LAST // 2, LAST)):
-            copy(
-                out=y_bf_last[:, a:b, :].rearrange("p (c i) t -> p c t i", i=RUN),
-                in_=y_last[:, :, a:b].rearrange("p t (c i) -> p c t i", i=RUN),
-            )
+        nc.vector.tensor_tensor(y_last[:, PACK - 1, :], back_end[:, PACK - 1, :], prod_end[:, PACK - 1, :], ADD)
+        nc.sync.dma_start(out=out_planes[:, PACK - 1, 2 * P : X], in_=y_end[:, PACK - 1, :])
+        quantise(y_bf[:], 0, 2 * P)
+        nc.sync.dma_start(out=out_words[:, 0 : 2 * P], in_=y_codes[:, 0 : 2 * P].bitcast(I32))
+        y_bf_last = keep.tile([P, LAST, PACK], BF16, name="y_bf", align_bytes=64)
+        nc.vector.tensor_copy(
+            out=y_bf_last[:].rearrange("p (c i) t -> p c t i", i=RUN),
+            in_=y_last.rearrange("p t (c i) -> p c t i", i=RUN),
+        )
+        quantise(y_bf_mid[:], 2 * P, P)
         quantise(y_bf_last[:], WIDE, LAST)
-        nc.sync.dma_start(out=out_words[:, WIDE:X], in_=y_codes[:, WIDE:X].bitcast(I32))
+        nc.sync.dma_start(out=out_words[:, 2 * P : X], in_=y_codes[:, 2 * P : X].bitcast(I32))
 
         for q in range(QUADS):
             queue = nc.sync if q % 2 == 0 else nc.scalar

@@ -24,6 +24,7 @@ LISTS = 4
 QUADS = 4
 N = 512
 PER_COLUMN = 16
+ALIGN = 256
 
 TAIL = 128
 DY_PIECES = ((256, 112), (256, 112), (256, 112), (TAIL, 64), (TAIL, 64))
@@ -41,19 +42,19 @@ def tile_attend_gupsamp_pl_kernel(
         keep = ctx.enter_context(tc.tile_pool(name="keep", bufs=1))
         psum = ctx.enter_context(tc.psum_pool(name="psum", bufs=1))
 
-        offs = [keep.tile([P, X // PER_COLUMN], U16, name="offs%d" % j) for j in range(LISTS)]
-        mat_words = keep.tile([P, 2 * D], U8, name="mat_words", align_bytes=64)
-        mat_scales = keep.tile([P, D], U8, name="mat_scales", align_bytes=64)
-        dealt_words = keep.tile([P, 2 * D], U8, name="dealt_words", align_bytes=64)
-        dealt_scales = keep.tile([P, D], U8, name="dealt_scales", align_bytes=64)
-        ident = keep.tile([P, P], F32, name="ident")
+        offs = [keep.tile([P, X // PER_COLUMN], U16, name="offs%d" % j, align_bytes=ALIGN) for j in range(LISTS)]
+        mat_words = keep.tile([P, 2 * D], U8, name="mat_words", align_bytes=ALIGN)
+        mat_scales = keep.tile([P, D], U8, name="mat_scales", align_bytes=ALIGN)
+        dealt_words = keep.tile([P, 2 * D], U8, name="dealt_words", align_bytes=ALIGN)
+        dealt_scales = keep.tile([P, D], U8, name="dealt_scales", align_bytes=ALIGN)
+        ident = keep.tile([P, P], F32, name="ident", align_bytes=ALIGN)
 
         nc.gpsimd.memset(mat_scales[:].bitcast(I32), 0)
         nc.sync.dma_start(out=mat_words[:].bitcast(I32), in_=W_words[0].bitcast(I32))
         pieces = []
         s0 = 0
         for k, (width, on_scalar) in enumerate(DY_PIECES):
-            raw = keep.tile([P, PACK, width], F32, name="stage%d" % k)
+            raw = keep.tile([P, PACK, width], F32, name="stage%d" % k, align_bytes=ALIGN)
             nc.sync.dma_start(out=raw[:], in_=dyT[:, s0 : s0 + width].rearrange("(p j) w -> p j w", j=PACK))
             pieces.append((raw, s0, width, width - on_scalar))
             s0 = s0 + width
@@ -78,10 +79,10 @@ def tile_attend_gupsamp_pl_kernel(
                 in_=mat_scales[:].rearrange("p (q t) -> p t q", t=PACK)[:, t, :],
             )
 
-        dy_codes = keep.tile([P, S], U32, name="dy_codes", align_bytes=64)
-        dy_scales = keep.tile([P, S], U8, name="dy_scales", align_bytes=64)
+        dy_codes = keep.tile([P, S], U32, name="dy_codes", align_bytes=ALIGN)
+        dy_scales = keep.tile([P, S], U8, name="dy_scales", align_bytes=ALIGN)
         for k, (raw, s0, width, cut) in enumerate(pieces):
-            dy_bf = keep.tile([P, width, PACK], BF16, name="dy_bf%d" % k, align_bytes=64)
+            dy_bf = keep.tile([P, width, PACK], BF16, name="dy_bf%d" % k, align_bytes=ALIGN)
             for copy, a, b in ((nc.vector.tensor_copy, 0, cut), (nc.scalar.copy, cut, width)):
                 copy(
                     out=dy_bf[:, a:b, :].rearrange("p (c i) j -> p c j i", i=RUN),
@@ -98,7 +99,7 @@ def tile_attend_gupsamp_pl_kernel(
         deal_scales(2)
         deal_scales(3)
 
-        u = [keep.tile([P, S], F32, name="stage%d" % (len(pieces) - 1))]
+        u = [keep.tile([P, S], F32, name="stage%d" % (len(pieces) - 1), align_bytes=ALIGN)]
 
         def mx_pass(t, first, bank_name):
             bank = psum.tile([P, N], F32, name=bank_name)
@@ -123,14 +124,14 @@ def tile_attend_gupsamp_pl_kernel(
         }
 
         def copy_plane(t, name):
-            plane = keep.tile([P, S], F32, name=name)
+            plane = keep.tile([P, S], F32, name=name, align_bytes=ALIGN)
             for h, bank in enumerate(later[t]):
                 nc.scalar.copy(out=plane[:, N * h : N * (h + 1)], in_=bank[:])
             u.append(plane)
 
         weights = []
         for k, pair in enumerate(((w0, w1), (w2, w3))):
-            both = keep.tile([P, len(pair), X], F32, name="stage%d" % k)
+            both = keep.tile([P, len(pair), X], F32, name="stage%d" % k, align_bytes=ALIGN)
             for e, w in enumerate(pair):
                 nc.sync.dma_start(out=both[:, e, :], in_=w)
                 weights.append(both[:, e, :])
@@ -157,7 +158,7 @@ def tile_attend_gupsamp_pl_kernel(
                 places.extend((bank, c, final) for c in range(count))
             for j in range(LISTS):
                 count = len(places) if j < LISTS - 1 else min(len(places), WIDE // P - c0)
-                prod = keep.tile([P, count * P], F32, name="prod%d_%d_%d" % (c0, t, j))
+                prod = keep.tile([P, count * P], F32, name="prod%d_%d_%d" % (c0, t, j), align_bytes=ALIGN)
                 product(prod[:], t, j, c0 * P, count * P)
                 for i in range(count):
                     bank, c, final = places[i]
@@ -175,18 +176,18 @@ def tile_attend_gupsamp_pl_kernel(
 
         def turn_back(t, c0, turned, banks):
             chunks = turned.shape[1]
-            summed = keep.tile([P, chunks, P], F32, name="summed%d_%d" % (c0, t))
+            summed = keep.tile([P, chunks, P], F32, name="summed%d_%d" % (c0, t), align_bytes=ALIGN)
             nc.scalar.copy(out=summed[:], in_=turned[:])
             for c in range(chunks):
                 nc.tensor.transpose(banks[c0 + c][:, t, :], summed[:, c, :], ident[:])
 
         backs = [psum.tile([P, PACK, P], F32, name="back%d" % c) for c in range(X // P)]
-        y_wide = keep.tile([P, PACK - 1, WIDE], F32, name="y_wide")
-        y_half = keep.tile([P, 2 * P], F32, name="y_half")
-        y_end = keep.tile([P, PACK, 2 * P], F32, name="y_end")
+        y_wide = keep.tile([P, PACK - 1, WIDE], F32, name="y_wide", align_bytes=ALIGN)
+        y_half = keep.tile([P, 2 * P], F32, name="y_half", align_bytes=ALIGN)
+        y_end = keep.tile([P, PACK, 2 * P], F32, name="y_end", align_bytes=ALIGN)
         y_last = y_end[:, :, P : 2 * P]
-        y_bf = keep.tile([P, 2 * P, PACK], BF16, name="y_bf", align_bytes=64)
-        y_bf_mid = keep.tile([P, P, PACK], BF16, name="y_bf_mid", align_bytes=64)
+        y_bf = keep.tile([P, 2 * P, PACK], BF16, name="y_bf", align_bytes=ALIGN)
+        y_bf_mid = keep.tile([P, P, PACK], BF16, name="y_bf_mid", align_bytes=ALIGN)
 
         def round_chunk(c):
             rounded = y_bf[:, P * c : P * (c + 1), :] if c < 2 else y_bf_mid[:]
@@ -214,14 +215,14 @@ def tile_attend_gupsamp_pl_kernel(
         nc.scalar.copy(out=y_end[:, t, 0:P], in_=backs[2][:, t, :])
         round_chunk(2)
 
-        prod_end = keep.tile([P, PACK, LAST], F32, name="summed0_3")
+        prod_end = keep.tile([P, PACK, LAST], F32, name="summed0_3", align_bytes=ALIGN)
         for t in range(PACK):
             product(prod_end[:, t, :], t, LISTS - 1, WIDE, LAST)
         nc.vector.tensor_tensor(y_last[:, 0:3, :], backs[-1][:, 0:3, :], prod_end[:, 0:3, :], ADD)
         nc.sync.dma_start(out=out_planes[:, 0 : PACK - 1, WIDE:X], in_=y_last[:, 0 : PACK - 1, :])
 
-        y_codes = keep.tile([P, X], U32, name="y_codes", align_bytes=64)
-        y_scales = keep.tile([P, X], U8, name="y_scales", align_bytes=64)
+        y_codes = keep.tile([P, X], U32, name="y_codes", align_bytes=ALIGN)
+        y_scales = keep.tile([P, X], U8, name="y_scales", align_bytes=ALIGN)
 
         def quantise(rounded, x0, width):
             nc.vector.quantize_mx(
@@ -234,7 +235,7 @@ def tile_attend_gupsamp_pl_kernel(
         nc.sync.dma_start(out=out_planes[:, PACK - 1, 2 * P : X], in_=y_end[:, PACK - 1, :])
         quantise(y_bf[:], 0, 2 * P)
         nc.sync.dma_start(out=out_words[:, 0 : 2 * P], in_=y_codes[:, 0 : 2 * P].bitcast(I32))
-        y_bf_last = keep.tile([P, LAST, PACK], BF16, name="y_bf", align_bytes=64)
+        y_bf_last = keep.tile([P, LAST, PACK], BF16, name="y_bf", align_bytes=ALIGN)
         nc.vector.tensor_copy(
             out=y_bf_last[:].rearrange("p (c i) t -> p c t i", i=RUN),
             in_=y_last.rearrange("p t (c i) -> p c t i", i=RUN),

@@ -17,6 +17,7 @@ E4M3 = mybir.dt.float8_e4m3fn_x4
 E2M1 = mybir.dt.float4_e2m1fn_x4
 MULT = mybir.AluOpType.mult
 ADD = mybir.AluOpType.add
+COPY = mybir.ActivationFunctionType.Copy
 
 P = 128
 PACK = 4
@@ -27,9 +28,10 @@ PER_COLUMN = 16
 ALIGN = 256
 
 TAIL = 128
-DY_PIECES = ((256, 112), (256, 112), (256, 112), (TAIL, 64), (TAIL, 64))
+DY_PIECES = ((TAIL, 64), (256, 112), (256, 112), (256, 112), (TAIL, 64))
 RUN = 4
 
+RING = 3
 LAST = P
 WIDE = X - LAST
 
@@ -81,6 +83,18 @@ def tile_attend_gupsamp_pl_kernel(
 
         dy_codes = keep.tile([P, S], U32, name="dy_codes", align_bytes=ALIGN)
         dy_scales = keep.tile([P, S], U8, name="dy_scales", align_bytes=ALIGN)
+
+        def mx_pass(t, out, s0, width):
+            nc.tensor.matmul_mx(
+                out=out,
+                lhsT=dealt_words[:, 2 * P * t : 2 * P * (t + 1)].bitcast(E2M1),
+                lhsT_scale=dealt_scales[:, P * t : P * (t + 1)],
+                rhs=dy_codes[:, s0 : s0 + width].bitcast(E5M2),
+                rhs_scale=dy_scales[:, s0 : s0 + width],
+                start=True,
+                stop=True,
+            )
+
         for k, (raw, s0, width, cut) in enumerate(pieces):
             dy_bf = keep.tile([P, width, PACK], BF16, name="dy_bf%d" % k, align_bytes=ALIGN)
             for copy, a, b in ((nc.vector.tensor_copy, 0, cut), (nc.scalar.copy, cut, width)):
@@ -99,150 +113,186 @@ def tile_attend_gupsamp_pl_kernel(
         deal_scales(2)
         deal_scales(3)
 
-        u = [keep.tile([P, S], F32, name="stage%d" % (len(pieces) - 1), align_bytes=ALIGN)]
+        u = [
+            keep.tile([P, S], F32, name=name, align_bytes=ALIGN)
+            for name in ("stage%d" % (len(pieces) - 2), "dy_bf%d" % (len(pieces) - 1), "u2")
+        ]
+        banks = [psum.tile([P, N - TAIL], F32, name="b0")]
+        mx_pass(0, banks[0][:, 0:TAIL], 0, TAIL)
+        mx_pass(0, banks[0][:, TAIL : N - TAIL], TAIL, N // 2)
+        nc.scalar.copy(out=u[0][:, 0 : N - TAIL], in_=banks[0][:])
+        for (raw, s0, width, cut), name in zip(pieces[2:], ("b1", "b6", "b2")):
+            bank = psum.tile([P, width], F32, name=name)
+            mx_pass(0, bank[:], s0, width)
+            nc.scalar.copy(out=u[0][:, s0 : s0 + width], in_=bank[:])
+        halves = {}
+        for t, names in ((1, ("b3", "b4")), (2, ("b2", "b7")), (3, ("b6", "b3"))):
+            for h, name in enumerate(names):
+                halves[t, h] = psum.tile([P, N], F32, name=name)
+                mx_pass(t, halves[t, h][:], N * h, N)
+                if (t, h) == (1, 0):
+                    nc.vector.tensor_copy(out=u[1][:, 0:N], in_=halves[1, 0][:])
 
-        def mx_pass(t, first, bank_name):
-            bank = psum.tile([P, N], F32, name=bank_name)
-            nc.tensor.matmul_mx(
-                out=bank[:],
-                lhsT=dealt_words[:, 2 * P * t : 2 * P * (t + 1)].bitcast(E2M1),
-                lhsT_scale=dealt_scales[:, P * t : P * (t + 1)],
-                rhs=dy_codes[:, first : first + N].bitcast(E5M2),
-                rhs_scale=dy_scales[:, first : first + N],
-                start=True,
-                stop=True,
-            )
-            return bank
+        def copy_u(t, h):
+            nc.scalar.copy(out=u[t][:, N * h : N * (h + 1)], in_=halves[t, h][:])
 
-        banks = [mx_pass(0, 0, "turn2"), mx_pass(0, N - 2 * TAIL, "turn3"), mx_pass(0, N, "turn1")]
-        nc.scalar.copy(out=u[0][:, 0:N], in_=banks[0][:])
-        nc.vector.tensor_copy(out=u[0][:, N : S - 2 * TAIL], in_=banks[1][:, 2 * TAIL : N])
-        nc.scalar.copy(out=u[0][:, S - 2 * TAIL : S], in_=banks[2][:, N - 2 * TAIL : N])
-        later = {
-            t: [mx_pass(t, N * h, name) for h, name in enumerate(names)]
-            for t, names in ((1, ("back0", "back1")), (2, ("back2", "back3")), (3, ("turn2", "turn3")))
-        }
-
-        def copy_plane(t, name):
-            plane = keep.tile([P, S], F32, name=name, align_bytes=ALIGN)
-            for h, bank in enumerate(later[t]):
-                nc.scalar.copy(out=plane[:, N * h : N * (h + 1)], in_=bank[:])
-            u.append(plane)
-
-        weights = []
-        for k, pair in enumerate(((w0, w1), (w2, w3))):
+        weights = {}
+        for k, pair in enumerate((((0, w0), (3, w3)), ((2, w2), (1, w1)))):
             both = keep.tile([P, len(pair), X], F32, name="stage%d" % k, align_bytes=ALIGN)
-            for e, w in enumerate(pair):
+            for e, (j, w) in enumerate(pair):
                 nc.sync.dma_start(out=both[:, e, :], in_=w)
-                weights.append(both[:, e, :])
+                weights[j] = both[:, e, :]
+        w_down = keep.tile([P, X // P], F32, name="stage2", align_bytes=ALIGN)
+        with nc.allow_non_contiguous_dma(reason="one weight to a partition"):
+            nc.sync.dma_start(out=w_down[:], in_=w1[0].rearrange("(c p) -> p c", p=P))
 
         out_planes = out_0.rearrange("(p t) x -> p t x", t=PACK)
         out_words = out_1[0].rearrange("p x t -> p (x t)").bitcast(I32)
 
-        def product(out, t, j, x0, width):
-            nc.vector.tensor_tensor(
-                out,
-                u[t][:].indirect(offs[j][:, x0 // PER_COLUMN : (x0 + width) // PER_COLUMN]),
-                weights[j][:, x0 : x0 + width],
-                MULT,
+        def window(t, j, x0, width):
+            return u[t][:].indirect(offs[j][:, x0 // PER_COLUMN : (x0 + width) // PER_COLUMN])
+
+        made = []
+
+        plain = {}
+
+        def ring(name=None):
+            if name is None:
+                name = "prod%d" % (len(made) % RING)
+                made.append(name)
+            return keep.tile([P, X], F32, name=name, align_bytes=ALIGN)
+
+        def product(prod, t, j, x0, width):
+            source = plain[t, j][:, x0 : x0 + width] if (t, j) in plain else window(t, j, x0, width)
+            nc.vector.tensor_tensor(prod[:, x0 : x0 + width], source, weights[j][:, x0 : x0 + width], MULT)
+
+        def plane_sum(t, names, order, closing=None):
+            size = 4 // len(names)
+            sums = [psum.tile([P, size, P], F32, name=name) for name in names]
+            for j in order:
+                prod = ring(closing if j == order[-1] else None)
+                step = size * P if j == order[-1] else X
+                for x0 in range(0, X, step):
+                    product(prod, t, j, x0, step)
+                    for c in range(x0 // P, (x0 + step) // P):
+                        nc.tensor.matmul(
+                            sums[c // size][:, c % size, :],
+                            prod[:, P * c : P * (c + 1)],
+                            ident[:],
+                            start=(j == order[0] and c % size == 0),
+                            stop=(j == order[-1] and c % size == size - 1),
+                            is_transpose=True,
+                        )
+            return sums
+
+        def pick_plain(t, j, into):
+            plain[t, j] = into
+            nc.scalar.activation(into, window(t, j, 0, X), COPY)
+
+        def turn_back(name, turned, summed):
+            bank = psum.tile([P, turned.shape[1], P], F32, name=name)
+            nc.scalar.copy(out=summed, in_=turned[:])
+            for i in range(turned.shape[1]):
+                nc.tensor.transpose(bank[:, i, :], summed[:, i, :], ident[:])
+            return bank
+
+        def pick(t, into, pair_banks):
+            nc.scalar.activation(into, window(t, 1, 0, X), COPY)
+            for c in range(4):
+                nc.tensor.transpose(pair_banks[c // 2][:, c % 2, t % 2, :], into[:, P * c : P * (c + 1)], ident[:])
+
+        def weigh(pair_banks, name):
+            out = []
+            for c in range(4):
+                out.append(keep.tile([P, 2, P], F32, name="%s%d" % (name, c), align_bytes=ALIGN))
+                nc.scalar.activation(out[c][:], pair_banks[c // 2][:, c % 2, :, :], COPY, scale=w_down[:, c : c + 1])
+            return out
+
+        def open_back(name, t, weighed, chunks):
+            bank = psum.tile([P, len(chunks), P], F32, name=name)
+            for i, c in enumerate(chunks):
+                nc.tensor.matmul(
+                    bank[:, i, :], weighed[c][:, t % 2, :], ident[:], start=(i == 0), stop=False, is_transpose=True
+                )
+            return bank
+
+        def close_back(bank, turned, summed):
+            count = turned.shape[1]
+            nc.scalar.copy(out=summed, in_=turned[:])
+            for i in range(count):
+                nc.tensor.matmul(
+                    bank[:, i, :], summed[:, i, :], ident[:], start=False, stop=(i == count - 1), is_transpose=True
+                )
+
+        def room(name, count):
+            return keep.tile([P, count, P], F32, name=name, align_bytes=ALIGN)[:]
+
+        def finish(t, bank):
+            nc.scalar.copy(out=y[:, t, :], in_=bank[:].rearrange("p c x -> p (c x)"))
+            nc.sync.dma_start(out=out_planes[:, t, :], in_=y[:, t, :])
+
+        low = [psum.tile([P, 2, 2, P], F32, name=name) for name in ("b0", "b1")]
+        picked0 = keep.tile([P, X], F32, name="picked0", align_bytes=ALIGN)
+        picked1 = keep.tile([P, X], F32, name="picked1", align_bytes=ALIGN)
+        pick(0, picked0[:], low)
+        copy_u(1, 1)
+        (sum0,) = plane_sum(0, ("b5",), (0, 3, 2), "closing0")
+        pick(1, picked1[:], low)
+        copy_u(2, 0)
+        copy_u(2, 1)
+        pick_plain(2, 1, keep.tile([P, X], F32, name="picked2", align_bytes=ALIGN)[:])
+        weighed = weigh(low, "low")
+        back0 = open_back("b2", 0, weighed, range(4))
+        close_back(back0, sum0, room("summed0", 4))
+        (sum1,) = plane_sum(1, ("b4",), (0, 3, 2), "closing1")
+        back1 = open_back("b0", 1, weighed, range(4))
+        u.append(keep.tile([P, S], F32, name="closing0", align_bytes=ALIGN))
+        copy_u(3, 0)
+        copy_u(3, 1)
+        (sum2,) = plane_sum(2, ("b7",), (0, 1, 2), "closing2")
+        both = keep.tile([P, 2, X], F32, name="closing1", align_bytes=ALIGN)
+        pick_plain(3, 1, both[:, 0, :])
+        pick_plain(3, 2, both[:, 1, :])
+        sums3 = plane_sum(3, ("b5", "b6"), (0, 1, 2))
+        close_back(back1, sum1, room("summed1", 4))
+        back2 = turn_back("b1", sum2, room("summed2", 4))
+        back3 = [turn_back(name, sums3[h], room("summed3_%d" % h, 2)) for h, name in enumerate(("b3", "b4"))]
+        y = keep.tile([P, PACK, X], F32, name="closing2", align_bytes=ALIGN)
+        finish(0, back0)
+        finish(1, back1)
+        ends = {2: ring(made[-3]), 3: ring(made[-2])}
+        product(ends[2], 2, 3, 0, X)
+        product(ends[3], 3, 3, 0, X)
+        nc.vector.tensor_tensor(y[:, 2, :], back2[:].rearrange("p c x -> p (c x)"), ends[2][:], ADD)
+        nc.sync.dma_start(out=out_planes[:, 2, :], in_=y[:, 2, :])
+        t = PACK - 1
+        for h in range(2):
+            half = slice(2 * P * h, 2 * P * (h + 1))
+            nc.vector.tensor_tensor(y[:, t, half], back3[h][:].rearrange("p c x -> p (c x)"), ends[t][:, half], ADD)
+        nc.sync.dma_start(out=out_planes[:, t, :], in_=y[:, t, :])
+
+        def round_y(copy, rounded, source):
+            copy(
+                out=rounded.rearrange("p (c i) t -> p c t i", i=RUN),
+                in_=source.rearrange("p t (c i) -> p c t i", i=RUN),
             )
 
-        def plane_sum(t, c0, groups):
-            places = []
-            turned = []
-            for name, count in groups:
-                bank = psum.tile([P, count, P], F32, name=name)
-                turned.append(bank)
-                first = c0 + len(places)
-                final = max((LISTS - 1 if first + c < WIDE // P else LISTS - 2, c) for c in range(count))
-                places.extend((bank, c, final) for c in range(count))
-            for j in range(LISTS):
-                count = len(places) if j < LISTS - 1 else min(len(places), WIDE // P - c0)
-                prod = keep.tile([P, count * P], F32, name="prod%d_%d_%d" % (c0, t, j), align_bytes=ALIGN)
-                product(prod[:], t, j, c0 * P, count * P)
-                for i in range(count):
-                    bank, c, final = places[i]
-                    nc.tensor.matmul(
-                        bank[:, c, :],
-                        prod[:, P * i : P * (i + 1)],
-                        ident[:],
-                        start=(j == 0 and c == 0),
-                        stop=((j, c) == final),
-                        is_transpose=True,
-                    )
-                if t == 0 and j < PACK - 1:
-                    copy_plane(j + 1, "prod0_0_%d" % j)
-            return turned
-
-        def turn_back(t, c0, turned, banks):
-            chunks = turned.shape[1]
-            summed = keep.tile([P, chunks, P], F32, name="summed%d_%d" % (c0, t), align_bytes=ALIGN)
-            nc.scalar.copy(out=summed[:], in_=turned[:])
-            for c in range(chunks):
-                nc.tensor.transpose(banks[c0 + c][:, t, :], summed[:, c, :], ident[:])
-
-        backs = [psum.tile([P, PACK, P], F32, name="back%d" % c) for c in range(X // P)]
-        y_wide = keep.tile([P, PACK - 1, WIDE], F32, name="y_wide", align_bytes=ALIGN)
-        y_half = keep.tile([P, 2 * P], F32, name="y_half", align_bytes=ALIGN)
-        y_end = keep.tile([P, PACK, 2 * P], F32, name="y_end", align_bytes=ALIGN)
-        y_last = y_end[:, :, P : 2 * P]
-        y_bf = keep.tile([P, 2 * P, PACK], BF16, name="y_bf", align_bytes=ALIGN)
-        y_bf_mid = keep.tile([P, P, PACK], BF16, name="y_bf_mid", align_bytes=ALIGN)
-
-        def round_chunk(c):
-            rounded = y_bf[:, P * c : P * (c + 1), :] if c < 2 else y_bf_mid[:]
-            nc.scalar.copy(out=rounded, in_=backs[c][:].rearrange("p t x -> p x t"))
-
-        for t in range(PACK - 1):
-            groups = (("turn%d" % t, 4),) if t < 2 else (("turn2", 2), ("turn3", 2))
-            for g, turned in enumerate(plane_sum(t, 0, groups)):
-                turn_back(t, 2 * g, turned, backs)
-            for c in range(WIDE // P):
-                nc.scalar.copy(out=y_wide[:, t, P * c : P * (c + 1)], in_=backs[c][:, t, :])
-            nc.sync.dma_start(out=out_planes[:, t, 0:WIDE], in_=y_wide[:, t, :])
-        t = PACK - 1
-        for c, turned in enumerate(plane_sum(t, 0, (("turn0", 1), ("turn1", 1)))):
-            turn_back(t, c, turned, backs)
-        turned = plane_sum(t, 2, (("turn2", 1), ("turn3", 1)))
-        for c in range(2):
-            nc.scalar.copy(out=y_half[:, P * c : P * (c + 1)], in_=backs[c][:, t, :])
-        nc.sync.dma_start(out=out_planes[:, t, 0 : 2 * P], in_=y_half[:])
-        round_chunk(0)
-        back_end = psum.tile([P, PACK, P], F32, name="turn0")
-        turn_back(t, 3, turned[1], backs[:-1] + [back_end])
-        turn_back(t, 2, turned[0], backs)
-        round_chunk(1)
-        nc.scalar.copy(out=y_end[:, t, 0:P], in_=backs[2][:, t, :])
-        round_chunk(2)
-
-        prod_end = keep.tile([P, PACK, LAST], F32, name="summed0_3", align_bytes=ALIGN)
-        for t in range(PACK):
-            product(prod_end[:, t, :], t, LISTS - 1, WIDE, LAST)
-        nc.vector.tensor_tensor(y_last[:, 0:3, :], backs[-1][:, 0:3, :], prod_end[:, 0:3, :], ADD)
-        nc.sync.dma_start(out=out_planes[:, 0 : PACK - 1, WIDE:X], in_=y_last[:, 0 : PACK - 1, :])
+        y_bf = [keep.tile([P, 2 * P, PACK], BF16, name=name, align_bytes=ALIGN) for name in ("summed3_1", "y_bf")]
+        for h in range(2):
+            round_y(nc.scalar.copy, y_bf[h][:, 0:P, :], y[:, :, 2 * P * h : 2 * P * h + P])
+        for h in range(2):
+            round_y(nc.vector.tensor_copy, y_bf[h][:, P : 2 * P, :], y[:, :, 2 * P * h + P : 2 * P * (h + 1)])
 
         y_codes = keep.tile([P, X], U32, name="y_codes", align_bytes=ALIGN)
         y_scales = keep.tile([P, X], U8, name="y_scales", align_bytes=ALIGN)
-
-        def quantise(rounded, x0, width):
+        for h in range(2):
+            half = slice(2 * P * h, 2 * P * (h + 1))
             nc.vector.quantize_mx(
-                out=y_codes[:, x0 : x0 + width].bitcast(E4M3),
-                scales=y_scales[:, x0 : x0 + width],
-                in_=rounded.rearrange("p x t -> p (x t)"),
+                out=y_codes[:, half].bitcast(E4M3),
+                scales=y_scales[:, half],
+                in_=y_bf[h][:].rearrange("p x t -> p (x t)"),
             )
-
-        nc.vector.tensor_tensor(y_last[:, PACK - 1, :], back_end[:, PACK - 1, :], prod_end[:, PACK - 1, :], ADD)
-        nc.sync.dma_start(out=out_planes[:, PACK - 1, 2 * P : X], in_=y_end[:, PACK - 1, :])
-        quantise(y_bf[:], 0, 2 * P)
-        nc.sync.dma_start(out=out_words[:, 0 : 2 * P], in_=y_codes[:, 0 : 2 * P].bitcast(I32))
-        y_bf_last = keep.tile([P, LAST, PACK], BF16, name="y_bf", align_bytes=ALIGN)
-        nc.vector.tensor_copy(
-            out=y_bf_last[:].rearrange("p (c i) t -> p c t i", i=RUN),
-            in_=y_last.rearrange("p t (c i) -> p c t i", i=RUN),
-        )
-        quantise(y_bf_mid[:], 2 * P, P)
-        quantise(y_bf_last[:], WIDE, LAST)
-        nc.sync.dma_start(out=out_words[:, 2 * P : X], in_=y_codes[:, 2 * P : X].bitcast(I32))
+            nc.sync.dma_start(out=out_words[:, half], in_=y_codes[:, half].bitcast(I32))
 
         for q in range(QUADS):
             queue = nc.sync if q % 2 == 0 else nc.scalar

from contextlib import ExitStack

import concourse.mybir as mybir
from concourse.masks import make_identity

M, D, X, S = 512, 512, 512, 1024
FLOPS = 2 * M * D * S

F32 = mybir.dt.float32
BF16 = mybir.dt.bfloat16
I32 = mybir.dt.int32
U32 = mybir.dt.uint32
U16 = mybir.dt.uint16
U8 = mybir.dt.uint8
E5M2 = mybir.dt.float8_e5m2_x4
E4M3 = mybir.dt.float8_e4m3fn_x4
E2M1 = mybir.dt.float4_e2m1fn_x4
MULT = mybir.AluOpType.mult
ADD = mybir.AluOpType.add
COPY = mybir.ActivationFunctionType.Copy

P = 128
PACK = 4
LISTS = 4
QUADS = 4
N = 512
PER_COLUMN = 16
ALIGN = 256

TAIL = 128
DY_PIECES = ((TAIL, 64), (256, 112), (256, 112), (256, 112), (TAIL, 64))
RUN = 4

RING = 3
LAST = P
WIDE = X - LAST


def tile_attend_gupsamp_pl_kernel(
    tc, W_words, W_scales, dyT, w0, w1, w2, w3, f0offs, f1offs, f2offs, f3offs, out_0, out_1, out_2
):
    nc = tc.nc
    with ExitStack() as ctx:
        keep = ctx.enter_context(tc.tile_pool(name="keep", bufs=1))
        psum = ctx.enter_context(tc.psum_pool(name="psum", bufs=1))

        offs = [keep.tile([P, X // PER_COLUMN], U16, name="offs%d" % j, align_bytes=ALIGN) for j in range(LISTS)]
        mat_words = keep.tile([P, 2 * D], U8, name="mat_words", align_bytes=ALIGN)
        mat_scales = keep.tile([P, D], U8, name="mat_scales", align_bytes=ALIGN)
        dealt_words = keep.tile([P, 2 * D], U8, name="dealt_words", align_bytes=ALIGN)
        dealt_scales = keep.tile([P, D], U8, name="dealt_scales", align_bytes=ALIGN)
        ident = keep.tile([P, P], F32, name="ident", align_bytes=ALIGN)

        nc.gpsimd.memset(mat_scales[:].bitcast(I32), 0)
        nc.sync.dma_start(out=mat_words[:].bitcast(I32), in_=W_words[0].bitcast(I32))
        pieces = []
        s0 = 0
        for k, (width, on_scalar) in enumerate(DY_PIECES):
            raw = keep.tile([P, PACK, width], F32, name="stage%d" % k, align_bytes=ALIGN)
            nc.sync.dma_start(out=raw[:], in_=dyT[:, s0 : s0 + width].rearrange("(p j) w -> p j w", j=PACK))
            pieces.append((raw, s0, width, width - on_scalar))
            s0 = s0 + width
            if k == 0:
                for q in range(QUADS):
                    nc.sync.dma_start(
                        out=mat_scales[32 * q : 32 * q + 4, :].bitcast(I32),
                        in_=W_scales[0, 4 * q : 4 * q + 4, :].bitcast(I32),
                    )
        for j, f in enumerate((f0offs, f1offs, f2offs, f3offs)):
            nc.sync.dma_start(offs[j][:], f)
        make_identity(nc, ident[:])

        nc.vector.tensor_copy(
            out=dealt_words[:].bitcast(U16).rearrange("p (t q) -> p t q", t=PACK),
            in_=mat_words[:].bitcast(U16).rearrange("p (q t) -> p t q", t=PACK),
        )

        def deal_scales(t):
            nc.vector.tensor_copy(
                out=dealt_scales[:, P * t : P * (t + 1)],
                in_=mat_scales[:].rearrange("p (q t) -> p t q", t=PACK)[:, t, :],
            )

        dy_codes = keep.tile([P, S], U32, name="dy_codes", align_bytes=ALIGN)
        dy_scales = keep.tile([P, S], U8, name="dy_scales", align_bytes=ALIGN)

        def mx_pass(t, out, s0, width):
            nc.tensor.matmul_mx(
                out=out,
                lhsT=dealt_words[:, 2 * P * t : 2 * P * (t + 1)].bitcast(E2M1),
                lhsT_scale=dealt_scales[:, P * t : P * (t + 1)],
                rhs=dy_codes[:, s0 : s0 + width].bitcast(E5M2),
                rhs_scale=dy_scales[:, s0 : s0 + width],
                start=True,
                stop=True,
            )

        for k, (raw, s0, width, cut) in enumerate(pieces):
            dy_bf = keep.tile([P, width, PACK], BF16, name="dy_bf%d" % k, align_bytes=ALIGN)
            for copy, a, b in ((nc.vector.tensor_copy, 0, cut), (nc.scalar.copy, cut, width)):
                copy(
                    out=dy_bf[:, a:b, :].rearrange("p (c i) j -> p c j i", i=RUN),
                    in_=raw[:, :, a:b].rearrange("p j (c i) -> p c j i", i=RUN),
                )
            nc.vector.quantize_mx(
                out=dy_codes[:, s0 : s0 + width].bitcast(E5M2),
                scales=dy_scales[:, s0 : s0 + width],
                in_=dy_bf[:].rearrange("p w j -> p (w j)"),
            )
            if k == 0:
                deal_scales(0)
                deal_scales(1)
        deal_scales(2)
        deal_scales(3)

        u = [
            keep.tile([P, S], F32, name=name, align_bytes=ALIGN)
            for name in ("stage%d" % (len(pieces) - 2), "dy_bf%d" % (len(pieces) - 1), "u2")
        ]
        banks = [psum.tile([P, N - TAIL], F32, name="b0")]
        mx_pass(0, banks[0][:, 0:TAIL], 0, TAIL)
        mx_pass(0, banks[0][:, TAIL : N - TAIL], TAIL, N // 2)
        nc.scalar.copy(out=u[0][:, 0 : N - TAIL], in_=banks[0][:])
        for (raw, s0, width, cut), name in zip(pieces[2:], ("b1", "b6", "b2")):
            bank = psum.tile([P, width], F32, name=name)
            mx_pass(0, bank[:], s0, width)
            nc.scalar.copy(out=u[0][:, s0 : s0 + width], in_=bank[:])
        halves = {}
        for t, names in ((1, ("b3", "b4")), (2, ("b2", "b7")), (3, ("b6", "b3"))):
            for h, name in enumerate(names):
                halves[t, h] = psum.tile([P, N], F32, name=name)
                mx_pass(t, halves[t, h][:], N * h, N)
                if (t, h) == (1, 0):
                    nc.vector.tensor_copy(out=u[1][:, 0:N], in_=halves[1, 0][:])

        def copy_u(t, h):
            nc.scalar.copy(out=u[t][:, N * h : N * (h + 1)], in_=halves[t, h][:])

        weights = {}
        for k, pair in enumerate((((0, w0), (3, w3)), ((2, w2), (1, w1)))):
            both = keep.tile([P, len(pair), X], F32, name="stage%d" % k, align_bytes=ALIGN)
            for e, (j, w) in enumerate(pair):
                nc.sync.dma_start(out=both[:, e, :], in_=w)
                weights[j] = both[:, e, :]
        w_down = keep.tile([P, X // P], F32, name="stage2", align_bytes=ALIGN)
        with nc.allow_non_contiguous_dma(reason="one weight to a partition"):
            nc.sync.dma_start(out=w_down[:], in_=w1[0].rearrange("(c p) -> p c", p=P))

        out_planes = out_0.rearrange("(p t) x -> p t x", t=PACK)
        out_words = out_1[0].rearrange("p x t -> p (x t)").bitcast(I32)

        def window(t, j, x0, width):
            return u[t][:].indirect(offs[j][:, x0 // PER_COLUMN : (x0 + width) // PER_COLUMN])

        made = []

        plain = {}

        def ring(name=None):
            if name is None:
                name = "prod%d" % (len(made) % RING)
                made.append(name)
            return keep.tile([P, X], F32, name=name, align_bytes=ALIGN)

        def product(prod, t, j, x0, width):
            source = plain[t, j][:, x0 : x0 + width] if (t, j) in plain else window(t, j, x0, width)
            nc.vector.tensor_tensor(prod[:, x0 : x0 + width], source, weights[j][:, x0 : x0 + width], MULT)

        def plane_sum(t, names, order, closing=None):
            size = 4 // len(names)
            sums = [psum.tile([P, size, P], F32, name=name) for name in names]
            for j in order:
                prod = ring(closing if j == order[-1] else None)
                step = size * P if j == order[-1] else X
                for x0 in range(0, X, step):
                    product(prod, t, j, x0, step)
                    for c in range(x0 // P, (x0 + step) // P):
                        nc.tensor.matmul(
                            sums[c // size][:, c % size, :],
                            prod[:, P * c : P * (c + 1)],
                            ident[:],
                            start=(j == order[0] and c % size == 0),
                            stop=(j == order[-1] and c % size == size - 1),
                            is_transpose=True,
                        )
            return sums

        def pick_plain(t, j, into):
            plain[t, j] = into
            nc.scalar.activation(into, window(t, j, 0, X), COPY)

        def turn_back(name, turned, summed):
            bank = psum.tile([P, turned.shape[1], P], F32, name=name)
            nc.scalar.copy(out=summed, in_=turned[:])
            for i in range(turned.shape[1]):
                nc.tensor.transpose(bank[:, i, :], summed[:, i, :], ident[:])
            return bank

        def pick(t, into, pair_banks):
            nc.scalar.activation(into, window(t, 1, 0, X), COPY)
            for c in range(4):
                nc.tensor.transpose(pair_banks[c // 2][:, c % 2, t % 2, :], into[:, P * c : P * (c + 1)], ident[:])

        def weigh(pair_banks, name):
            out = []
            for c in range(4):
                out.append(keep.tile([P, 2, P], F32, name="%s%d" % (name, c), align_bytes=ALIGN))
                nc.scalar.activation(out[c][:], pair_banks[c // 2][:, c % 2, :, :], COPY, scale=w_down[:, c : c + 1])
            return out

        def open_back(name, t, weighed, chunks):
            bank = psum.tile([P, len(chunks), P], F32, name=name)
            for i, c in enumerate(chunks):
                nc.tensor.matmul(
                    bank[:, i, :], weighed[c][:, t % 2, :], ident[:], start=(i == 0), stop=False, is_transpose=True
                )
            return bank

        def close_back(bank, turned, summed):
            count = turned.shape[1]
            nc.scalar.copy(out=summed, in_=turned[:])
            for i in range(count):
                nc.tensor.matmul(
                    bank[:, i, :], summed[:, i, :], ident[:], start=False, stop=(i == count - 1), is_transpose=True
                )

        def room(name, count):
            return keep.tile([P, count, P], F32, name=name, align_bytes=ALIGN)[:]

        def finish(t, bank):
            nc.scalar.copy(out=y[:, t, :], in_=bank[:].rearrange("p c x -> p (c x)"))
            nc.sync.dma_start(out=out_planes[:, t, :], in_=y[:, t, :])

        low = [psum.tile([P, 2, 2, P], F32, name=name) for name in ("b0", "b1")]
        picked0 = keep.tile([P, X], F32, name="picked0", align_bytes=ALIGN)
        picked1 = keep.tile([P, X], F32, name="picked1", align_bytes=ALIGN)
        pick(0, picked0[:], low)
        copy_u(1, 1)
        (sum0,) = plane_sum(0, ("b5",), (0, 3, 2), "closing0")
        pick(1, picked1[:], low)
        copy_u(2, 0)
        copy_u(2, 1)
        pick_plain(2, 1, keep.tile([P, X], F32, name="picked2", align_bytes=ALIGN)[:])
        weighed = weigh(low, "low")
        back0 = open_back("b2", 0, weighed, range(4))
        close_back(back0, sum0, room("summed0", 4))
        (sum1,) = plane_sum(1, ("b4",), (0, 3, 2), "closing1")
        back1 = open_back("b0", 1, weighed, range(4))
        u.append(keep.tile([P, S], F32, name="closing0", align_bytes=ALIGN))
        copy_u(3, 0)
        copy_u(3, 1)
        (sum2,) = plane_sum(2, ("b7",), (0, 1, 2), "closing2")
        both = keep.tile([P, 2, X], F32, name="closing1", align_bytes=ALIGN)
        pick_plain(3, 1, both[:, 0, :])
        pick_plain(3, 2, both[:, 1, :])
        sums3 = plane_sum(3, ("b5", "b6"), (0, 1, 2))
        close_back(back1, sum1, room("summed1", 4))
        back2 = turn_back("b1", sum2, room("summed2", 4))
        back3 = [turn_back(name, sums3[h], room("summed3_%d" % h, 2)) for h, name in enumerate(("b3", "b4"))]
        y = keep.tile([P, PACK, X], F32, name="closing2", align_bytes=ALIGN)
        finish(0, back0)
        finish(1, back1)
        ends = {2: ring(made[-3]), 3: ring(made[-2])}
        product(ends[2], 2, 3, 0, X)
        product(ends[3], 3, 3, 0, X)
        nc.vector.tensor_tensor(y[:, 2, :], back2[:].rearrange("p c x -> p (c x)"), ends[2][:], ADD)
        nc.sync.dma_start(out=out_planes[:, 2, :], in_=y[:, 2, :])
        t = PACK - 1
        for h in range(2):
            half = slice(2 * P * h, 2 * P * (h + 1))
            nc.vector.tensor_tensor(y[:, t, half], back3[h][:].rearrange("p c x -> p (c x)"), ends[t][:, half], ADD)
        nc.sync.dma_start(out=out_planes[:, t, :], in_=y[:, t, :])

        def round_y(copy, rounded, source):
            copy(
                out=rounded.rearrange("p (c i) t -> p c t i", i=RUN),
                in_=source.rearrange("p t (c i) -> p c t i", i=RUN),
            )

        y_bf = [keep.tile([P, 2 * P, PACK], BF16, name=name, align_bytes=ALIGN) for name in ("summed3_1", "y_bf")]
        for h in range(2):
            round_y(nc.scalar.copy, y_bf[h][:, 0:P, :], y[:, :, 2 * P * h : 2 * P * h + P])
        for h in range(2):
            round_y(nc.vector.tensor_copy, y_bf[h][:, P : 2 * P, :], y[:, :, 2 * P * h + P : 2 * P * (h + 1)])

        y_codes = keep.tile([P, X], U32, name="y_codes", align_bytes=ALIGN)
        y_scales = keep.tile([P, X], U8, name="y_scales", align_bytes=ALIGN)
        for h in range(2):
            half = slice(2 * P * h, 2 * P * (h + 1))
            nc.vector.quantize_mx(
                out=y_codes[:, half].bitcast(E4M3),
                scales=y_scales[:, half],
                in_=y_bf[h][:].rearrange("p x t -> p (x t)"),
            )
            nc.sync.dma_start(out=out_words[:, half], in_=y_codes[:, half].bitcast(I32))

        for q in range(QUADS):
            queue = nc.sync if q % 2 == 0 else nc.scalar
            queue.dma_start(
                out=out_2[0, 4 * q : 4 * q + 4, :].bitcast(I32),
                in_=y_scales[32 * q : 32 * q + 4, :].bitcast(I32),
            )
